import numpy as np
import ml_dtypes


def mxq(x, axis, fmt="e4m3"):
    dtype, down = {"e4m3": (ml_dtypes.float8_e4m3fn, 7), "e5m2": (ml_dtypes.float8_e5m2, 14)}[fmt]
    v = np.moveaxis(np.asarray(x, np.float32).astype(ml_dtypes.bfloat16).astype(np.float64), axis, -1)
    blocks = v.reshape(v.shape[:-1] + (-1, 32))
    amax = np.abs(blocks).max(-1, keepdims=True)
    byte = np.maximum(np.where(amax > 0, np.frexp(amax)[1] - 1 + 127, 0) - down, 1)
    scale = np.exp2(byte - 127.0)
    codes = (blocks / scale).astype(np.float32).astype(dtype).astype(np.float64)
    return np.moveaxis((codes * scale).reshape(v.shape), -1, axis)


WIDE = False


def mx_kscale(k):
    if not WIDE:
        return np.ones(k)
    levels = np.array([10, -10, 5, -5, 0])
    if k % 512:
        return np.exp2(np.random.permutation(np.resize(levels, k // 32))).repeat(32)
    a = np.empty((k // 512, 16))
    for p in range(k // 512):
        a[p, :8] = np.random.permutation(np.resize(levels, 8))
        for g in range(8):
            far = levels[np.abs(levels - a[p, g]) >= 10]
            a[p, g + 8] = far[np.random.randint(len(far))]
    return np.exp2(a.ravel()).repeat(32)


BF16 = ml_dtypes.bfloat16


def bf(x):
    return np.asarray(x, np.float32).astype(BF16)


def f64(x):
    return np.asarray(x).astype(np.float64)


E2M1 = np.array([0.0, 0.5, 1.0, 1.5, 2.0, 3.0, 4.0, 6.0, -0.0, -0.5, -1.0, -1.5, -2.0, -3.0, -4.0, -6.0])


def pack_weight(w, fmt):
    k, n = w.shape
    w = f64(bf(w)).reshape(k // 32, 32, n)
    amax = np.abs(w).max(1)
    if fmt == "e4m3":
        byte = np.frexp(amax)[1] - 1 + 127 - 7
    else:
        mant, ex = np.frexp(amax / 6.0)
        byte = np.where(mant > 0.5, ex, ex - 1) + 127
    byte = np.clip(np.where(amax > 0, byte, 1), 1, 254)
    scaled = (w * np.exp2(127.0 - byte)[:, None, :]).reshape(k, n).astype(np.float32)
    by_word = np.ascontiguousarray(scaled.reshape(k // 512, 128, 4, n).transpose(0, 1, 3, 2))
    if fmt == "e4m3":
        words = by_word.astype(ml_dtypes.float8_e4m3fn).view(np.uint8)
    else:
        c = by_word.astype(ml_dtypes.float4_e2m1fn).view(np.uint8) & 0xF
        words = c[..., 0::2] | (c[..., 1::2] << 4)
    return np.ascontiguousarray(words), np.ascontiguousarray(byte.astype(np.uint8).reshape(k // 512, 16, n))


def unpack_weight(words, scales, fmt):
    g, p, n, _ = words.shape
    if fmt == "e4m3":
        vals = np.ascontiguousarray(words).view(ml_dtypes.float8_e4m3fn).astype(np.float64)
    else:
        nib = np.empty((g, p, n, 4), np.uint8)
        nib[..., 0::2] = words & 0xF
        nib[..., 1::2] = words >> 4
        vals = E2M1[nib]
    vals = vals * np.repeat(np.exp2(scales.astype(np.float64) - 127.0), 8, axis=1)[..., None]
    return vals.transpose(0, 1, 3, 2).reshape(g * 512, n)
def pack4(w):
    words, scales = pack_weight(w, "e2m1")
    return words.reshape(words.shape[0], 128, -1), scales


def unpack4(words, scales):
    return unpack_weight(words.reshape(words.shape[0], 128, -1, 2), scales, "e2m1")


def planes(Y):
    n, m = Y.shape
    b = f64(bf(Y)).reshape(n // 32, 32, m)
    amax = np.abs(b).max(1)
    byte = np.clip(np.where(amax > 0, np.frexp(amax)[1] - 1 + 127 - 7, 1), 1, 254)
    codes = (b * np.exp2(127.0 - byte)[:, None, :]).reshape(n, m).astype(np.float32).astype(ml_dtypes.float8_e4m3fn).view(np.uint8)
    words = codes.reshape(n // 512, 128, 4, m).transpose(0, 1, 3, 2)
    return np.ascontiguousarray(words), np.ascontiguousarray(byte.astype(np.uint8).reshape(n // 512, 16, m))


T, D, N, Q = 1024, 1024, 1024, 1024


def setup_inputs():
    s, t = mx_kscale(D), mx_kscale(T)
    z = bf(np.random.standard_normal((T, D)) * s)
    wo_words, wo_scales = pack4(np.random.standard_normal((D, N)) / np.sqrt(D) / s[:, None])
    wg_words, wg_scales = pack4(np.random.standard_normal((D, Q)) / np.sqrt(D) / s[:, None])
    return {"z": z,
            "wo_words": wo_words,
            "wo_scales": wo_scales,
            "wg_words": wg_words,
            "wg_scales": wg_scales,
            "bg": bf(np.random.standard_normal(Q) * 0.5),
            "r": bf(np.random.standard_normal((T, N))),
            "v": bf((1.0 + 0.1 * np.random.standard_normal(T)) * t),
            "u": bf((1.0 + 0.1 * np.random.standard_normal(T)) / t)}


def stochastic_discount_factor(zq, wo, r):
    om = zq @ wo
    return 1.0 - (1.0 / np.sqrt(N)) * np.sum(om * r, axis=1)


def weighted_test_functions(zq, wg, bg, u):
    return u[:, None] * np.tanh((zq @ wg) + bg[None, :])


def core(z, wo_words, wo_scales, wg_words, wg_scales, bg, r, v, u):
    rr = f64(r)
    zq = mxq(f64(z), 1, "e4m3")
    sdf = stochastic_discount_factor(zq, unpack4(wo_words, wo_scales), rr)
    f = weighted_test_functions(zq, unpack4(wg_words, wg_scales), f64(bg), f64(u))
    d = (f64(v) * sdf)[:, None] * rr
    return (1.0 / np.sqrt(T)) * (mxq(d, 0, "e4m3").T @ mxq(f, 0, "e4m3"))


def reference(z, wo_words, wo_scales, wg_words, wg_scales, bg, r, v, u):
    R_out = core(z, wo_words, wo_scales, wg_words, wg_scales, bg, r, v, u)
    words, scales = planes(R_out.T)
    return R_out, words, scales

@@ -1,0 +1,437 @@
+from contextlib import ExitStack
+
+import concourse.mybir as mybir
+from concourse.masks import make_identity
+
+F32 = mybir.dt.float32
+BF16 = mybir.dt.bfloat16
+U8 = mybir.dt.uint8
+U32 = mybir.dt.uint32
+I32 = mybir.dt.int32
+E4M3 = mybir.dt.float8_e4m3fn_x4
+E2M1 = mybir.dt.float4_e2m1fn_x4
+ADD = mybir.AluOpType.add
+MULT = mybir.AluOpType.mult
+ACT = mybir.ActivationFunctionType
+
+T, D, N, Q = 1024, 1024, 1024, 1024
+FLOPS = 3 * 2 * 1024 * 1024 * 1024
+
+
+def tile_adversarialsdfconditionalpricingmoments_x2_kernel(
+    tc, z, wo_words, wo_scales, wg_words, wg_scales, bg, r, v, u, out_0, out_1, out_2
+):
+    nc = tc.nc
+    with ExitStack() as ctx:
+        keep = ctx.enter_context(tc.tile_pool(name="keep", bufs=1))
+        work = ctx.enter_context(tc.tile_pool(name="work", bufs=4))
+        psum = ctx.enter_context(tc.psum_pool(name="psum", bufs=4))
+        ctx.enter_context(tc.manual_schedule())
+
+        def kt(name, shape, dtype):
+            return keep.tile(shape, dtype, name=name, align_bytes=64)
+
+        ident = kt("ident", [128, 128], F32)
+        z_sb = [kt("z%d" % g, [128, 4, D], BF16) for g in range(2)]
+        r_sb = [kt("r%d" % g, [128, 4, N], BF16) for g in range(2)]
+        w_sb = {k: kt("w" + k, [128, 2, 2 * N], U8) for k in "og"}
+        ws_sb = {k: kt("ws" + k, [128, 2, N], U8) for k in "og"}
+        bg_rows = kt("bg_rows", [128, 128], BF16)
+        bg_f = kt("bg_f", [128, 128], F32)
+        bg_t = kt("bg_t", [128, 8], F32)
+        v_sb = kt("v", [128, 2, 4], BF16)
+        u_sb = kt("u", [128, 2, 4], BF16)
+        warm = kt("warm", [128, 1], F32)
+        zin = [[kt("zin%d%d" % (g, h), [128, 512, 4], BF16) for h in range(2)] for g in range(2)]
+        zc = [[kt("zc%d%d" % (g, h), [128, 512], U32) for h in range(2)] for g in range(2)]
+        zs = [[kt("zs%d%d" % (g, h), [128, 512], U8) for h in range(2)] for g in range(2)]
+        fin = [kt("fin%d" % g, [128, Q, 4], BF16) for g in range(2)]
+        fc = [kt("fc%d" % g, [128, Q], U32) for g in range(2)]
+        fs = [kt("fs%d" % g, [128, Q], U8) for g in range(2)]
+        dsc = [kt("dsc%d" % g, [128, 4, N], BF16) for g in range(2)]
+        din = [kt("din%d" % g, [128, N, 4], BF16) for g in range(2)]
+        dc = [kt("dc%d" % g, [128, N], U32) for g in range(2)]
+        ds = [kt("ds%d" % g, [128, N], U8) for g in range(2)]
+        acc = [kt("acc%d" % g, [128, 4, 2], F32) for g in range(2)]
+        sv = [kt("sv%d" % g, [128, 3, 4], F32) for g in range(2)]
+        pin = [kt("pin%d" % h, [128, N, 4], BF16) for h in range(2)]
+        pc = [kt("pc%d" % h, [128, N], U32) for h in range(2)]
+        ps = [kt("ps%d" % h, [128, N], U8) for h in range(2)]
+
+        for k in "go":
+            nc.vector.memset(ws_sb[k][:].rearrange("p g n -> p (g n)").bitcast(I32), 0)
+        nc.vector.memset(bg_rows[:], 0.0)
+        nc.vector.memset(warm[:], 0.0)
+        nc.scalar.activation(out=warm[:], in_=warm[:], func=ACT.Tanh)
+
+        def load_z(g, half):
+            nc.sync.dma_start(
+                out=z_sb[g][:, 2 * half : 2 * half + 2, :],
+                in_=z[512 * g : 512 * (g + 1), :].rearrange("(p j) d -> p j d", j=4)[:, 2 * half : 2 * half + 2, :],
+            )
+
+        def load_scales(eng, k, src):
+            for b in range(4):
+                eng.dma_start(
+                    out=ws_sb[k][32 * b : 32 * b + 4, :, :].bitcast(I32),
+                    in_=src[:, 4 * b : 4 * b + 4, :].rearrange("g q n -> q g n").bitcast(I32),
+                )
+
+        def load_words(k, src):
+            nc.sync.dma_start(out=w_sb[k][:].bitcast(I32), in_=src.rearrange("g p n -> p g n").bitcast(I32))
+
+        def load_r(g, half):
+            nc.sync.dma_start(
+                out=r_sb[g][:, 2 * half : 2 * half + 2, :],
+                in_=r[512 * g : 512 * (g + 1), :].rearrange("(p j) i -> p j i", j=4)[:, 2 * half : 2 * half + 2, :],
+            )
+
+        load_z(0, 0)
+        load_z(0, 1)
+        load_scales(nc.scalar, "o", wo_scales)
+        load_words("o", wo_words)
+        load_r(0, 0)
+        load_r(0, 1)
+        load_words("g", wg_words)
+        load_z(1, 0)
+        load_z(1, 1)
+        load_r(1, 0)
+        load_r(1, 1)
+        make_identity(nc, ident[:])
+        nc.gpsimd.dma_start(out=bg_rows[0:8, :], in_=bg.rearrange("(a p) -> a p", p=128))
+        nc.gpsimd.dma_start(out=v_sb[:], in_=v.rearrange("(g p j) -> p g j", p=128, j=4))
+        nc.gpsimd.dma_start(out=u_sb[:], in_=u.rearrange("(g p j) -> p g j", p=128, j=4))
+        load_scales(nc.gpsimd, "g", wg_scales)
+
+        def bank(tag, shape):
+            return psum.tile(shape, F32, name=tag, tag=tag)
+
+        hold = {}
+
+        def zT(g, h, jp):
+            t = bank("tr", [128, 2, 256])
+            w = z_sb[g][:].rearrange("p j d -> p (j d)").bitcast(F32).rearrange("p (j w) -> p j w", j=4)
+            for e in range(2):
+                for jj in range(2):
+                    nc.tensor.transpose(
+                        t[:, e, 128 * jj : 128 * (jj + 1)],
+                        w[:, 2 * jp + jj, 256 * h + e : 256 * (h + 1) : 2],
+                        ident[:],
+                    )
+            hold["z", g, h, jp] = t
+
+        def zE(g, h, jp, eng):
+            o = zin[g][h][:, 256 * jp : 256 * (jp + 1), :].rearrange("p c k -> p (c k)").bitcast(F32).rearrange("p (c e) -> p c e", e=2)
+            i = hold["z", g, h, jp][:].rearrange("p e c -> p c e")
+            if eng == "S":
+                nc.scalar.copy(out=o, in_=i)
+            else:
+                nc.vector.tensor_copy(out=o, in_=i)
+
+        def zQ(g, h, c0, c1):
+            nc.vector.quantize_mx(
+                out=zc[g][h][:, c0:c1].bitcast(E4M3),
+                scales=zs[g][h][:, c0:c1],
+                in_=zin[g][h][:, c0:c1, :].rearrange("p c k -> p (c k)"),
+            )
+
+        def bgT():
+            nc.scalar.copy(out=bg_f[:], in_=bg_rows[:])
+            t = bank("tr", [128, 128])
+            nc.tensor.transpose(t[:], bg_f[:], ident[:])
+            nc.scalar.copy(out=bg_t[:], in_=t[:, 0:8])
+
+        def wgM(g, qt):
+            t = bank("mm", [128, 512])
+            for h in range(2):
+                nc.tensor.matmul_mx(
+                    out=t[:],
+                    lhsT=w_sb["g"][:, h, 256 * qt : 256 * (qt + 1)].bitcast(E2M1),
+                    lhsT_scale=ws_sb["g"][:, h, 128 * qt : 128 * (qt + 1)],
+                    rhs=zc[g][h][:].bitcast(E4M3),
+                    rhs_scale=zs[g][h][:],
+                    start=h == 0,
+                    stop=h == 1,
+                )
+            hold["x", g, qt] = t
+
+        def tanh(g, qt):
+            t = work.tile([128, 512], F32, name="th", bufs=16)
+            nc.scalar.activation(out=t[:], in_=hold["x", g, qt][:], func=ACT.Tanh, bias=bg_t[:, qt : qt + 1])
+            hold["t", g, qt] = t
+
+        def fT(g, qt):
+            t = bank("tr", [128, 4, 128])
+            for j in range(4):
+                nc.tensor.transpose(t[:, j, :], hold["t", g, qt][:, 128 * j : 128 * (j + 1)], ident[:])
+            hold["f", g, qt] = t
+
+        def fE(g, qt):
+            o = fin[g][:].rearrange("p (h j b a) k -> p h j b a k", h=2, j=4, b=4)
+            nc.vector.tensor_tensor(
+                out=o[:, qt // 4, :, qt % 4, :, :],
+                in0=hold["f", g, qt][:].rearrange("p k (a j) -> p j a k", j=4),
+                in1=u_sb[:, g, :].unsqueeze(1).unsqueeze(1).to_broadcast([128, 4, 32, 4]),
+                op=MULT,
+            )
+
+        def fQ(g, h):
+            c = slice(512 * h, 512 * (h + 1))
+            nc.vector.quantize_mx(
+                out=fc[g][:, c].bitcast(E4M3), scales=fs[g][:, c], in_=fin[g][:, c, :].rearrange("p c k -> p (c k)")
+            )
+
+        def omM(g, j, nh):
+            t = bank("mm", [128, 512])
+            for h in range(2):
+                nc.tensor.matmul_mx(
+                    out=t[:],
+                    lhsT=zc[g][h][:, 128 * j : 128 * (j + 1)].bitcast(E4M3),
+                    lhsT_scale=zs[g][h][:, 128 * j : 128 * (j + 1)],
+                    rhs=w_sb["o"][:, h, 1024 * nh : 1024 * (nh + 1)].bitcast(E2M1),
+                    rhs_scale=ws_sb["o"][:, h, 512 * nh : 512 * (nh + 1)],
+                    start=h == 0,
+                    stop=h == 1,
+                )
+            hold["o", g, j, nh] = t
+
+        def omR(g, j, nh):
+            junk = work.tile([128, 512], F32, name="junk", bufs=2)
+            nc.vector.scalar_tensor_tensor(
+                out=junk[:],
+                in0=hold["o", g, j, nh][:],
+                scalar=1.0,
+                in1=r_sb[g][:, j, 512 * nh : 512 * (nh + 1)],
+                op0=MULT,
+                op1=MULT,
+                accum_out=acc[g][:, j, nh : nh + 1],
+            )
+
+        def sd(g):
+            a, b, c = (sv[g][:, k, :] for k in range(3))
+            nc.vector.tensor_tensor(out=a, in0=acc[g][:, :, 0], in1=acc[g][:, :, 1], op=ADD)
+            nc.vector.tensor_scalar(out=b, in0=a, scalar1=-1.0 / 32, scalar2=1.0, op0=MULT, op1=ADD)
+            nc.vector.tensor_tensor(out=c, in0=b, in1=v_sb[:, g, :], op=MULT)
+
+        def dS(g, j, eng="V"):
+            a = dict(out=dsc[g][:, j, :], in0=r_sb[g][:, j, :], scalar1=sv[g][:, 2, j : j + 1], op0=MULT)
+            if eng == "V":
+                nc.vector.tensor_scalar(scalar2=None, **a)
+            else:
+                nc.gpsimd.tensor_scalar(scalar2=0.0, op1=ADD, **a)
+
+        def dI(g, c0, c1, eng="S"):
+            o, i = din[g][:, c0:c1, :], dsc[g][:, :, c0:c1].rearrange("p j c -> p c j")
+            if eng == "S":
+                nc.scalar.copy(out=o, in_=i)
+            else:
+                nc.vector.tensor_copy(out=o, in_=i)
+
+        def dQ(g, c0, c1):
+            nc.vector.quantize_mx(
+                out=dc[g][:, c0:c1].bitcast(E4M3), scales=ds[g][:, c0:c1], in_=din[g][:, c0:c1, :].rearrange("p c k -> p (c k)")
+            )
+
+        def outM(h, it):
+            t = bank("mm", [128, 512])
+            for g in range(2):
+                nc.tensor.matmul_mx(
+                    out=t[:],
+                    lhsT=dc[g][:, 128 * it : 128 * (it + 1)].bitcast(E4M3),
+                    lhsT_scale=ds[g][:, 128 * it : 128 * (it + 1)],
+                    rhs=fc[g][:, 512 * h : 512 * (h + 1)].bitcast(E4M3),
+                    rhs_scale=fs[g][:, 512 * h : 512 * (h + 1)],
+                    start=g == 0,
+                    stop=g == 1,
+                )
+            hold["out", h, it] = t
+
+        def outE(h, it, eng="S"):
+            t = work.tile([128, 512], F32, name="osb", bufs=8)
+            o = t[:].rearrange("p (c j) -> p c j", j=4)
+            i = hold["out", h, it][:].rearrange("p (j c) -> p c j", j=4)
+            if eng == "S":
+                nc.scalar.mul(out=o, in_=i, mul=1.0 / 32)
+            else:
+                nc.vector.tensor_scalar(out=o, in0=i, scalar1=1.0 / 32, scalar2=None, op0=MULT)
+            nc.sync.dma_start(out=out_0[128 * it : 128 * (it + 1), 512 * h : 512 * (h + 1)], in_=t[:])
+            hold["os", h, it] = t
+
+        def pB(h, it, eng="V"):
+            t = work.tile([128, 512], BF16, name="ob", bufs=8)
+            o = t[:].rearrange("p (w c e) -> p w c e", w=2, e=2)
+            i = hold["os", h, it][:].rearrange("p (c w e) -> p w c e", w=2, e=2)
+            if eng == "V":
+                nc.vector.tensor_copy(out=o, in_=i)
+            else:
+                nc.gpsimd.tensor_scalar(out=o, in0=i, scalar1=1.0, scalar2=0.0, op0=MULT, op1=ADD)
+            hold["ob", h, it] = t
+
+        def pT(h, ip):
+            t = bank("tr", [128, 2, 256])
+            for k in range(2):
+                w = hold["ob", h, 2 * ip + k][:].bitcast(F32)
+                for e in range(2):
+                    nc.tensor.transpose(t[:, e, 128 * k : 128 * (k + 1)], w[:, 128 * e : 128 * (e + 1)], ident[:])
+            hold["pt", h, ip] = t
+
+        def pE(h, ip, eng):
+            c = slice(256 * ip, 256 * (ip + 1))
+            o = pin[h][:, c, :].rearrange("p c k -> p (c k)").bitcast(F32).rearrange("p (c e) -> p c e", e=2)
+            i = hold["pt", h, ip][:].rearrange("p e c -> p c e")
+            if eng == "S":
+                nc.scalar.copy(out=o, in_=i)
+            else:
+                nc.vector.tensor_copy(out=o, in_=i)
+
+        def pM(h, it):
+            t = bank("tr", [128, 4, 128])
+            for j in range(4):
+                c = slice(512 * h + 128 * j, 512 * h + 128 * (j + 1))
+                for g in range(2):
+                    nc.tensor.matmul_mx(
+                        out=t[:, j, :],
+                        lhsT=fc[g][:, c].bitcast(E4M3),
+                        lhsT_scale=fs[g][:, c],
+                        rhs=dc[g][:, 128 * it : 128 * (it + 1)].bitcast(E4M3),
+                        rhs_scale=ds[g][:, 128 * it : 128 * (it + 1)],
+                        start=g == 0,
+                        stop=g == 1,
+                    )
+            hold["pm", h, it] = t
+
+        def pD(h, it, eng):
+            o = pin[h][:, 128 * it : 128 * (it + 1), :]
+            i = hold["pm", h, it][:].rearrange("p j c -> p c j")
+            if eng == "S":
+                nc.scalar.mul(out=o, in_=i, mul=1.0 / 32)
+            else:
+                nc.vector.tensor_scalar(out=o, in0=i, scalar1=1.0 / 32, scalar2=None, op0=MULT)
+
+        def pQ(h, c0, c1):
+            nc.vector.quantize_mx(
+                out=pc[h][:, c0:c1].bitcast(E4M3), scales=ps[h][:, c0:c1], in_=pin[h][:, c0:c1, :].rearrange("p c k -> p (c k)")
+            )
+
+        def pW(h, c0, c1):
+            nc.sync.dma_start(
+                out=out_1[h].rearrange("p m t -> p (m t)")[:, 4 * c0 : 4 * c1].bitcast(I32), in_=pc[h][:, c0:c1].bitcast(I32)
+            )
+
+        def pS(h, eng=None):
+            for b in range(4):
+                (eng or nc.sync).dma_start(
+                    out=out_2[h, 4 * b : 4 * b + 4, :].bitcast(I32), in_=ps[h][32 * b : 32 * b + 4, :].bitcast(I32)
+                )
+
+
+        for jp in range(2):
+            for h in range(2):
+                zT(0, h, jp)
+                zE(0, h, jp, "SV"[h])
+            for h in range(2):
+                zQ(0, h, 256 * jp, 256 * (jp + 1))
+        for k in range(8):
+            omM(0, k // 2, k % 2)
+            omR(0, k // 2, k % 2)
+            if k == 5:
+                bgT()
+        for jp in range(2):
+            for h in range(2):
+                zT(1, h, jp)
+                zE(1, h, jp, "S")
+            for h in range(2):
+                zQ(1, h, 256 * jp, 256 * (jp + 1))
+        sd(0)
+        wq = [(g, q) for g in range(2) for q in range(4)]
+        for k in range(8):
+            wgM(*wq[k])
+            tanh(*wq[k])
+            omM(1, k // 2, k % 2)
+            if k < 2:
+                dS(0, 2 * k)
+                dS(0, 2 * k + 1)
+            omR(1, k // 2, k % 2)
+            if k % 2 and k > 1:
+                for m in (k - 3, k - 2):
+                    fT(*wq[m])
+                for m in (k - 3, k - 2):
+                    fE(*wq[m])
+            if k % 2:
+                dI(0, 128 * (k - 1), 128 * (k + 1))
+        sd(1)
+        for j in range(4):
+            dS(1, j)
+        for m in (6, 7):
+            fT(*wq[m])
+        wq = [(g, q) for g in range(2) for q in range(4, 8)]
+        for k in range(2):
+            wgM(*wq[k])
+            tanh(*wq[k])
+        dI(1, 0, 256, "V")
+        dI(1, 256, 512)
+        for k in range(2, 4):
+            wgM(*wq[k])
+            tanh(*wq[k])
+        dI(1, 512, 768)
+        for m in (6, 7):
+            fE(g=1, qt=m - 4)
+        fQ(0, 0)
+        fQ(1, 0)
+        dQ(0, 0, 512)
+        dQ(1, 0, 256)
+        dQ(1, 256, 512)
+        for m in range(4):
+            fT(*wq[m])
+        for k in range(4, 8):
+            wgM(*wq[k])
+            tanh(*wq[k])
+        for m in range(4):
+            fE(*wq[m])
+        dI(1, 768, 1024, "V")
+        for it in range(4):
+            outM(0, it)
+            outE(0, it, "S")
+        dQ(0, 512, 1024)
+        dQ(1, 512, 1024)
+        for m in range(4, 8):
+            fT(*wq[m])
+            fE(*wq[m])
+        for it in range(4):
+            pB(0, it, "G")
+        for g in range(2):
+            fQ(g, 1)
+        for it in range(4, 8):
+            outM(0, it)
+            outE(0, it, "S")
+        for ip in range(2):
+            pT(0, ip)
+            pE(0, ip, "V")
+        for it in range(4):
+            outM(1, it)
+            pB(0, it + 4, "G")
+            outE(1, it, "S")
+        pQ(0, 0, 512)
+        for ip in range(2, 4):
+            pT(0, ip)
+            pE(0, ip, "V")
+        for it in range(4):
+            pB(1, it, "G")
+        pQ(0, 512, 1024)
+        pW(0, 0, 1024)
+        pS(0)
+        for it in range(4, 8):
+            pM(1, it)
+            pD(1, it, "V")
+        for it in range(4, 8):
+            outM(1, it)
+            outE(1, it, "S")
+            if it == 5:
+                for ip in range(2):
+                    pT(1, ip)
+                    pE(1, ip, "V")
+        pQ(1, 512, 1024)
+        pW(1, 512, 1024)
+        pQ(1, 0, 512)
+        pW(1, 0, 512)
+        pS(1)

@@ -64,10 +64,10 @@ def tile_adversarialsdfconditionalpricingmoments_x2_kernel(
         nc.vector.memset(warm[:], 0.0)
         nc.scalar.activation(out=warm[:], in_=warm[:], func=ACT.Tanh)
 
-        def load_z(g, half):
+        def load_z(g, j0, j1):
             nc.sync.dma_start(
-                out=z_sb[g][:, 2 * half : 2 * half + 2, :],
-                in_=z[512 * g : 512 * (g + 1), :].rearrange("(p j) d -> p j d", j=4)[:, 2 * half : 2 * half + 2, :],
+                out=z_sb[g][:, j0:j1, :],
+                in_=z[512 * g : 512 * (g + 1), :].rearrange("(p j) d -> p j d", j=4)[:, j0:j1, :],
             )
 
         def load_scales(eng, k, src):
@@ -77,8 +77,10 @@ def tile_adversarialsdfconditionalpricingmoments_x2_kernel(
                     in_=src[:, 4 * b : 4 * b + 4, :].rearrange("g q n -> q g n").bitcast(I32),
                 )
 
-        def load_words(k, src):
-            nc.sync.dma_start(out=w_sb[k][:].bitcast(I32), in_=src.rearrange("g p n -> p g n").bitcast(I32))
+        def load_words(k, src, c0, c1):
+            nc.sync.dma_start(
+                out=w_sb[k][:, :, c0:c1].bitcast(I32), in_=src.rearrange("g p n -> p g n")[:, :, c0:c1].bitcast(I32)
+            )
 
         def load_r(g, half):
             nc.sync.dma_start(
@@ -86,15 +88,17 @@ def tile_adversarialsdfconditionalpricingmoments_x2_kernel(
                 in_=r[512 * g : 512 * (g + 1), :].rearrange("(p j) i -> p j i", j=4)[:, 2 * half : 2 * half + 2, :],
             )
 
-        load_z(0, 0)
-        load_z(0, 1)
+        load_z(0, 0, 1)
+        load_z(0, 1, 2)
+        load_z(0, 2, 4)
         load_scales(nc.scalar, "o", wo_scales)
-        load_words("o", wo_words)
+        load_words("o", wo_words, 0, N)
         load_r(0, 0)
+        load_words("o", wo_words, N, 2 * N)
         load_r(0, 1)
-        load_words("g", wg_words)
-        load_z(1, 0)
-        load_z(1, 1)
+        load_words("g", wg_words, 0, 2 * N)
+        load_z(1, 0, 2)
+        load_z(1, 2, 4)
         load_r(1, 0)
         load_r(1, 1)
         make_identity(nc, ident[:])
@@ -111,8 +115,8 @@ def tile_adversarialsdfconditionalpricingmoments_x2_kernel(
         def zT(g, h, jp):
             t = bank("tr", [128, 2, 256])
             w = z_sb[g][:].rearrange("p j d -> p (j d)").bitcast(F32).rearrange("p (j w) -> p j w", j=4)
-            for e in range(2):
-                for jj in range(2):
+            for jj in range(2):
+                for e in range(2):
                     nc.tensor.transpose(
                         t[:, e, 128 * jj : 128 * (jj + 1)],
                         w[:, 2 * jp + jj, 256 * h + e : 256 * (h + 1) : 2],
@@ -325,6 +329,7 @@ def tile_adversarialsdfconditionalpricingmoments_x2_kernel(
                 )
 
 
+        om = [(j, nh) for nh in range(2) for j in range(4)]
         for jp in range(2):
             for h in range(2):
                 zT(0, h, jp)
@@ -332,8 +337,8 @@ def tile_adversarialsdfconditionalpricingmoments_x2_kernel(
             for h in range(2):
                 zQ(0, h, 256 * jp, 256 * (jp + 1))
         for k in range(8):
-            omM(0, k // 2, k % 2)
-            omR(0, k // 2, k % 2)
+            omM(0, *om[k])
+            omR(0, *om[k])
             if k == 5:
                 bgT()
         for jp in range(2):
@@ -347,11 +352,11 @@ def tile_adversarialsdfconditionalpricingmoments_x2_kernel(
         for k in range(8):
             wgM(*wq[k])
             tanh(*wq[k])
-            omM(1, k // 2, k % 2)
+            omM(1, *om[k])
             if k < 2:
                 dS(0, 2 * k)
                 dS(0, 2 * k + 1)
-            omR(1, k // 2, k % 2)
+            omR(1, *om[k])
             if k % 2 and k > 1:
                 for m in (k - 3, k - 2):
                     fT(*wq[m])
@@ -362,32 +367,32 @@ def tile_adversarialsdfconditionalpricingmoments_x2_kernel(
         sd(1)
         for j in range(4):
             dS(1, j)
+        wr = [(g, q) for g in range(2) for q in range(4, 8)]
+        for k in range(2):
+            wgM(*wr[k])
+            tanh(*wr[k])
         for m in (6, 7):
             fT(*wq[m])
-        wq = [(g, q) for g in range(2) for q in range(4, 8)]
-        for k in range(2):
-            wgM(*wq[k])
-            tanh(*wq[k])
         dI(1, 0, 256, "V")
         dI(1, 256, 512)
         for k in range(2, 4):
-            wgM(*wq[k])
-            tanh(*wq[k])
+            wgM(*wr[k])
+            tanh(*wr[k])
         dI(1, 512, 768)
         for m in (6, 7):
-            fE(g=1, qt=m - 4)
+            fE(*wq[m])
         fQ(0, 0)
         fQ(1, 0)
         dQ(0, 0, 512)
         dQ(1, 0, 256)
         dQ(1, 256, 512)
         for m in range(4):
-            fT(*wq[m])
+            fT(*wr[m])
         for k in range(4, 8):
-            wgM(*wq[k])
-            tanh(*wq[k])
+            wgM(*wr[k])
+            tanh(*wr[k])
         for m in range(4):
-            fE(*wq[m])
+            fE(*wr[m])
         dI(1, 768, 1024, "V")
         for it in range(4):
             outM(0, it)
@@ -395,43 +400,56 @@ def tile_adversarialsdfconditionalpricingmoments_x2_kernel(
         dQ(0, 512, 1024)
         dQ(1, 512, 1024)
         for m in range(4, 8):
-            fT(*wq[m])
-            fE(*wq[m])
-        for it in range(4):
-            pB(0, it, "G")
+            fT(*wr[m])
+            fE(*wr[m])
         for g in range(2):
             fQ(g, 1)
+        for it in range(4):
+            pB(0, it)
         for it in range(4, 8):
             outM(0, it)
             outE(0, it, "S")
+        for it in range(2):
+            outM(1, it)
+            outE(1, it, "S")
         for ip in range(2):
             pT(0, ip)
-            pE(0, ip, "V")
-        for it in range(4):
+            pE(0, ip, "S")
+        for it in range(4, 8):
+            pB(0, it)
+        for it in range(2, 4):
             outM(1, it)
-            pB(0, it + 4, "G")
             outE(1, it, "S")
         pQ(0, 0, 512)
+        pW(0, 0, 512)
         for ip in range(2, 4):
             pT(0, ip)
             pE(0, ip, "V")
         for it in range(4):
-            pB(1, it, "G")
-        pQ(0, 512, 1024)
-        pW(0, 0, 1024)
-        pS(0)
-        for it in range(4, 8):
+            pB(1, it)
+        for it in range(6, 8):
             pM(1, it)
-            pD(1, it, "V")
-        for it in range(4, 8):
+            pD(1, it, "SV"[it % 2])
+        for it in range(4, 6):
             outM(1, it)
             outE(1, it, "S")
-            if it == 5:
-                for ip in range(2):
-                    pT(1, ip)
-                    pE(1, ip, "V")
-        pQ(1, 512, 1024)
-        pW(1, 512, 1024)
+        pQ(0, 512, 1024)
+        pW(0, 512, 1024)
+        pS(0)
+        for it in range(4, 6):
+            pB(1, it)
+        for ip in range(2):
+            pT(1, ip)
+            pE(1, ip, "V")
+        outM(1, 6)
+        outE(1, 6, "S")
+        pT(1, 2)
+        pE(1, 2, "V")
+        pQ(1, 768, 1024)
         pQ(1, 0, 512)
+        pQ(1, 512, 768)
+        outM(1, 7)
+        outE(1, 7, "S")
         pW(1, 0, 512)
+        pW(1, 512, 1024)
         pS(1)

@@ -37,11 +37,14 @@ def tile_adversarialsdfconditionalpricingmoments_x2_kernel(
         w_sb = {k: kt("w" + k, [128, 2, 2 * N], U8) for k in "og"}
         ws_sb = {k: kt("ws" + k, [128, 2, N], U8) for k in "og"}
         bg_rows = kt("bg_rows", [128, 128], BF16)
-        bg_f = kt("bg_f", [128, 128], F32)
         bg_t = kt("bg_t", [128, 8], F32)
         v_sb = kt("v", [128, 2, 4], BF16)
-        u_sb = kt("u", [128, 2, 4], BF16)
+        u_row = kt("u_row", [128, T], BF16)
+        ones = kt("ones", [128, 128], BF16)
+        u_bc = kt("u_bc", [128, 2, 512], F32)
+        eye = kt("eye", [128, 8], BF16)
         warm = kt("warm", [128, 1], F32)
+        zero = kt("zero", [128, 512], BF16)
         zin = [[kt("zin%d%d" % (g, h), [128, 512, 4], BF16) for h in range(2)] for g in range(2)]
         zc = [[kt("zc%d%d" % (g, h), [128, 512], U32) for h in range(2)] for g in range(2)]
         zs = [[kt("zs%d%d" % (g, h), [128, 512], U8) for h in range(2)] for g in range(2)]
@@ -58,10 +61,13 @@ def tile_adversarialsdfconditionalpricingmoments_x2_kernel(
         pc = [kt("pc%d" % h, [128, N], U32) for h in range(2)]
         ps = [kt("ps%d" % h, [128, N], U8) for h in range(2)]
 
-        for k in "go":
+        nc.vector.memset(zero[:], 0.0)
+        for k in "og":
             nc.vector.memset(ws_sb[k][:].rearrange("p g n -> p (g n)").bitcast(I32), 0)
         nc.vector.memset(bg_rows[:], 0.0)
         nc.vector.memset(warm[:], 0.0)
+        nc.vector.memset(u_row[:], 0.0)
+        nc.vector.memset(ones[:], 1.0)
         nc.scalar.activation(out=warm[:], in_=warm[:], func=ACT.Tanh)
 
         def load_z(g, j0, j1):
@@ -82,29 +88,25 @@ def tile_adversarialsdfconditionalpricingmoments_x2_kernel(
                 out=w_sb[k][:, :, c0:c1].bitcast(I32), in_=src.rearrange("g p n -> p g n")[:, :, c0:c1].bitcast(I32)
             )
 
-        def load_r(g, half):
+        def load_r(g, j0, j1):
             nc.sync.dma_start(
-                out=r_sb[g][:, 2 * half : 2 * half + 2, :],
-                in_=r[512 * g : 512 * (g + 1), :].rearrange("(p j) i -> p j i", j=4)[:, 2 * half : 2 * half + 2, :],
+                out=r_sb[g][:, j0:j1, :],
+                in_=r[512 * g : 512 * (g + 1), :].rearrange("(p j) i -> p j i", j=4)[:, j0:j1, :],
             )
 
-        load_z(0, 0, 1)
-        load_z(0, 1, 2)
+        load_z(0, 0, 2)
         load_z(0, 2, 4)
         load_scales(nc.scalar, "o", wo_scales)
-        load_words("o", wo_words, 0, N)
-        load_r(0, 0)
-        load_words("o", wo_words, N, 2 * N)
-        load_r(0, 1)
+        load_words("o", wo_words, 0, 2 * N)
+        load_r(0, 0, 2)
+        load_r(0, 2, 4)
         load_words("g", wg_words, 0, 2 * N)
-        load_z(1, 0, 2)
-        load_z(1, 2, 4)
-        load_r(1, 0)
-        load_r(1, 1)
+        load_z(1, 0, 4)
+        load_r(1, 0, 4)
         make_identity(nc, ident[:])
         nc.gpsimd.dma_start(out=bg_rows[0:8, :], in_=bg.rearrange("(a p) -> a p", p=128))
         nc.gpsimd.dma_start(out=v_sb[:], in_=v.rearrange("(g p j) -> p g j", p=128, j=4))
-        nc.gpsimd.dma_start(out=u_sb[:], in_=u.rearrange("(g p j) -> p g j", p=128, j=4))
+        nc.gpsimd.dma_start(out=u_row[0:1, :], in_=u.unsqueeze(0))
         load_scales(nc.gpsimd, "g", wg_scales)
 
         def bank(tag, shape):
@@ -112,25 +114,29 @@ def tile_adversarialsdfconditionalpricingmoments_x2_kernel(
 
         hold = {}
 
-        def zT(g, h, jp):
-            t = bank("tr", [128, 2, 256])
+        def zT(g, h, j0, j1):
+            n = 128 * (j1 - j0)
+            t = bank("tr", [128, 2, n])
             w = z_sb[g][:].rearrange("p j d -> p (j d)").bitcast(F32).rearrange("p (j w) -> p j w", j=4)
-            for jj in range(2):
+            for j in range(j0, j1):
                 for e in range(2):
                     nc.tensor.transpose(
-                        t[:, e, 128 * jj : 128 * (jj + 1)],
-                        w[:, 2 * jp + jj, 256 * h + e : 256 * (h + 1) : 2],
-                        ident[:],
+                        t[:, e, 128 * (j - j0) : 128 * (j - j0 + 1)], w[:, j, 256 * h + e : 256 * (h + 1) : 2], ident[:]
                     )
-            hold["z", g, h, jp] = t
+            hold["z", g, h, j0] = t
 
-        def zE(g, h, jp, eng):
-            o = zin[g][h][:, 256 * jp : 256 * (jp + 1), :].rearrange("p c k -> p (c k)").bitcast(F32).rearrange("p (c e) -> p c e", e=2)
-            i = hold["z", g, h, jp][:].rearrange("p e c -> p c e")
+        def zE(g, h, j0, j1, eng):
+            o = zin[g][h][:, 128 * j0 : 128 * j1, :].rearrange("p c k -> p (c k)").bitcast(F32).rearrange("p (c e) -> p c e", e=2)
+            i = hold["z", g, h, j0][:].rearrange("p e c -> p c e")
             if eng == "S":
                 nc.scalar.copy(out=o, in_=i)
             else:
                 nc.vector.tensor_copy(out=o, in_=i)
+
+        def dummy(n):
+            for k in range(n):
+                t = bank("mm", [128, 512])
+                nc.tensor.matmul(t[:], zero[:, 0:128], zero[:], start=True, stop=True)
 
         def zQ(g, h, c0, c1):
             nc.vector.quantize_mx(
@@ -140,10 +146,10 @@ def tile_adversarialsdfconditionalpricingmoments_x2_kernel(
             )
 
         def bgT():
-            nc.scalar.copy(out=bg_f[:], in_=bg_rows[:])
-            t = bank("tr", [128, 128])
-            nc.tensor.transpose(t[:], bg_f[:], ident[:])
-            nc.scalar.copy(out=bg_t[:], in_=t[:, 0:8])
+            nc.scalar.copy(out=eye[:], in_=ident[:, 0:8])
+            t = bank("tr", [128, 8])
+            nc.tensor.matmul(t[:], bg_rows[:], eye[:], start=True, stop=True)
+            nc.scalar.copy(out=bg_t[:], in_=t[:])
 
         def wgM(g, qt):
             t = bank("mm", [128, 512])
@@ -160,24 +166,45 @@ def tile_adversarialsdfconditionalpricingmoments_x2_kernel(
             hold["x", g, qt] = t
 
         def tanh(g, qt):
-            t = work.tile([128, 512], F32, name="th", bufs=16)
+            t = work.tile([128, 512], F32, name="th", bufs=12)
             nc.scalar.activation(out=t[:], in_=hold["x", g, qt][:], func=ACT.Tanh, bias=bg_t[:, qt : qt + 1])
             hold["t", g, qt] = t
 
-        def fT(g, qt):
-            t = bank("tr", [128, 4, 128])
-            for j in range(4):
-                nc.tensor.transpose(t[:, j, :], hold["t", g, qt][:, 128 * j : 128 * (j + 1)], ident[:])
-            hold["f", g, qt] = t
+        def uB():
+            for g in range(2):
+                t = bank("tr", [128, 512])
+                nc.tensor.matmul(t[:], ones[:], u_row[:, 512 * g : 512 * (g + 1)], start=True, stop=True)
+                nc.scalar.copy(
+                    out=u_bc[:, g, :].rearrange("p (w c e) -> p w c e", w=2, e=2),
+                    in_=t[:].rearrange("p (c w e) -> p w c e", w=2, e=2),
+                )
 
-        def fE(g, qt):
-            o = fin[g][:].rearrange("p (h j b a) k -> p h j b a k", h=2, j=4, b=4)
-            nc.vector.tensor_tensor(
-                out=o[:, qt // 4, :, qt % 4, :, :],
-                in0=hold["f", g, qt][:].rearrange("p k (a j) -> p j a k", j=4),
-                in1=u_sb[:, g, :].unsqueeze(1).unsqueeze(1).to_broadcast([128, 4, 32, 4]),
+        def fU(g, qt, eng="V"):
+            t = work.tile([128, 512], BF16, name="fb", bufs=8)
+            (nc.vector if eng == "V" else nc.gpsimd).tensor_tensor(
+                out=t[:].rearrange("p (w c e) -> p w c e", w=2, e=2),
+                in0=hold["t", g, qt][:].rearrange("p (w e c) -> p w c e", w=2, e=2),
+                in1=u_bc[:, g, :].rearrange("p (w c e) -> p w c e", w=2, e=2),
                 op=MULT,
             )
+            hold["b", g, qt] = t
+
+        def fT(g, qp):
+            t = bank("tr", [128, 2, 256])
+            for k in range(2):
+                w = hold["b", g, 2 * qp + k][:].bitcast(F32)
+                for e in range(2):
+                    nc.tensor.transpose(t[:, e, 128 * k : 128 * (k + 1)], w[:, 128 * e : 128 * (e + 1)], ident[:])
+            hold["f", g, qp] = t
+
+        def fE(g, qp, eng="S"):
+            w = fin[g][:].rearrange("p c k -> p (c k)").bitcast(F32).rearrange("p (h j b a e) -> p h j b a e", h=2, j=4, b=2, a=64)
+            o = w[:, qp // 2, :, qp % 2, :, :]
+            i = hold["f", g, qp][:].rearrange("p e (a j) -> p j a e", j=4)
+            if eng == "S":
+                nc.scalar.copy(out=o, in_=i)
+            else:
+                nc.vector.tensor_copy(out=o, in_=i)
 
         def fQ(g, h):
             c = slice(512 * h, 512 * (h + 1))
@@ -329,127 +356,128 @@ def tile_adversarialsdfconditionalpricingmoments_x2_kernel(
                 )
 
 
-        om = [(j, nh) for nh in range(2) for j in range(4)]
-        for jp in range(2):
+        dummy(6)
+        for j in (0, 2):
             for h in range(2):
-                zT(0, h, jp)
-                zE(0, h, jp, "SV"[h])
+                zT(0, h, j, j + 2)
+                zE(0, h, j, j + 2, "SV"[h])
             for h in range(2):
-                zQ(0, h, 256 * jp, 256 * (jp + 1))
+                zQ(0, h, 128 * j, 128 * (j + 2))
+        om = [(j, nh) for j in range(4) for nh in range(2)]
         for k in range(8):
             omM(0, *om[k])
             omR(0, *om[k])
-            if k == 5:
+            if k == 3:
                 bgT()
-        for jp in range(2):
-            for h in range(2):
-                zT(1, h, jp)
-                zE(1, h, jp, "S")
-            for h in range(2):
-                zQ(1, h, 256 * jp, 256 * (jp + 1))
+                uB()
         sd(0)
-        wq = [(g, q) for g in range(2) for q in range(4)]
-        for k in range(8):
-            wgM(*wq[k])
-            tanh(*wq[k])
-            omM(1, *om[k])
-            if k < 2:
-                dS(0, 2 * k)
-                dS(0, 2 * k + 1)
-            omR(1, *om[k])
-            if k % 2 and k > 1:
-                for m in (k - 3, k - 2):
-                    fT(*wq[m])
-                for m in (k - 3, k - 2):
-                    fE(*wq[m])
-            if k % 2:
-                dI(0, 128 * (k - 1), 128 * (k + 1))
+        for j in range(4):
+            dS(0, j)
+        for q in range(4):
+            wgM(0, q)
+            tanh(0, q)
+            fU(0, q, "G")
+        for j in (0, 2):
+            for h in range(2):
+                zT(1, h, j, j + 2)
+                zE(1, h, j, j + 2, "S")
+            for h in range(2):
+                zQ(1, h, 128 * j, 128 * (j + 2))
+        for k in range(4):
+            for i in (2 * k, 2 * k + 1):
+                omM(1, *om[i])
+                omR(1, *om[i])
+            wgM(1, k)
+            tanh(1, k)
+            fU(1, k, "G")
+            dI(0, 256 * k, 256 * (k + 1))
+            if k == 2:
+                fT(0, 0)
+                fT(0, 1)
+                fE(0, 0, "V")
+                fE(0, 1)
         sd(1)
         for j in range(4):
             dS(1, j)
-        wr = [(g, q) for g in range(2) for q in range(4, 8)]
-        for k in range(2):
-            wgM(*wr[k])
-            tanh(*wr[k])
-        for m in (6, 7):
-            fT(*wq[m])
+        for q in range(4, 8):
+            wgM(0, q)
+            tanh(0, q)
+            fU(0, q, "G")
         dI(1, 0, 256, "V")
-        dI(1, 256, 512)
-        for k in range(2, 4):
-            wgM(*wr[k])
-            tanh(*wr[k])
-        dI(1, 512, 768)
-        for m in (6, 7):
-            fE(*wq[m])
         fQ(0, 0)
-        fQ(1, 0)
+        dI(1, 256, 512, "V")
         dQ(0, 0, 512)
-        dQ(1, 0, 256)
-        dQ(1, 256, 512)
-        for m in range(4):
-            fT(*wr[m])
-        for k in range(4, 8):
-            wgM(*wr[k])
-            tanh(*wr[k])
-        for m in range(4):
-            fE(*wr[m])
+        dQ(1, 0, 512)
+        fT(1, 0)
+        fT(1, 1)
+        fE(1, 0)
+        fE(1, 1)
+        for q in range(4, 6):
+            wgM(1, q)
+            tanh(1, q)
+            fU(1, q, "G")
+        dI(1, 512, 768)
+        fQ(1, 0)
         dI(1, 768, 1024, "V")
-        for it in range(4):
-            outM(0, it)
-            outE(0, it, "S")
         dQ(0, 512, 1024)
-        dQ(1, 512, 1024)
-        for m in range(4, 8):
-            fT(*wr[m])
-            fE(*wr[m])
-        for g in range(2):
-            fQ(g, 1)
         for it in range(4):
-            pB(0, it)
+            outM(0, it)
+            outE(0, it, "VS"[it % 2])
+        for q in range(6, 8):
+            wgM(1, q)
+            tanh(1, q)
+            fU(1, q, "GV"[q % 2])
+        dQ(1, 512, 1024)
+        fT(0, 2)
+        fT(0, 3)
+        fE(0, 2, "V")
+        fE(0, 3, "V")
         for it in range(4, 8):
             outM(0, it)
             outE(0, it, "S")
-        for it in range(2):
-            outM(1, it)
-            outE(1, it, "S")
+        fQ(0, 1)
+        for it in range(4):
+            pB(0, it, "GV"[it % 2])
+        fT(1, 2)
+        fT(1, 3)
+        fE(1, 2, "V")
+        fE(1, 3, "V")
+        fQ(1, 1)
         for ip in range(2):
-            pT(0, ip)
-            pE(0, ip, "S")
-        for it in range(4, 8):
-            pB(0, it)
-        for it in range(2, 4):
-            outM(1, it)
-            outE(1, it, "S")
-        pQ(0, 0, 512)
-        pW(0, 0, 512)
-        for ip in range(2, 4):
             pT(0, ip)
             pE(0, ip, "V")
         for it in range(4):
-            pB(1, it)
-        for it in range(6, 8):
-            pM(1, it)
-            pD(1, it, "SV"[it % 2])
+            outM(1, it)
+            outE(1, it, "S")
+        for it in range(4, 8):
+            pB(0, it, "GV"[it % 2])
+        for ip in range(2, 4):
+            pT(0, ip)
+            pE(0, ip, "V")
+        pQ(0, 0, 512)
+        pW(0, 0, 512)
+        for it in range(4):
+            pB(1, it, "GV"[it % 2])
         for it in range(4, 6):
             outM(1, it)
             outE(1, it, "S")
         pQ(0, 512, 1024)
         pW(0, 512, 1024)
         pS(0)
+        for it in range(6, 8):
+            pM(1, it)
+            pD(1, it, "VS"[it % 2])
         for it in range(4, 6):
-            pB(1, it)
-        for ip in range(2):
+            pB(1, it, "V")
+        for ip in range(3):
             pT(1, ip)
-            pE(1, ip, "V")
-        outM(1, 6)
-        outE(1, 6, "S")
-        pT(1, 2)
-        pE(1, 2, "V")
+            pE(1, ip, "VSV"[ip])
         pQ(1, 768, 1024)
+        for it in range(6, 8):
+            outM(1, it)
+            outE(1, it, "S")
         pQ(1, 0, 512)
-        pQ(1, 512, 768)
-        outM(1, 7)
-        outE(1, 7, "S")
         pW(1, 0, 512)
+        pQ(1, 512, 768)
         pW(1, 512, 1024)
         pS(1)

@@ -26,7 +26,6 @@ def tile_adversarialsdfconditionalpricingmoments_x2_kernel(
         keep = ctx.enter_context(tc.tile_pool(name="keep", bufs=1))
         work = ctx.enter_context(tc.tile_pool(name="work", bufs=4))
         psum = ctx.enter_context(tc.psum_pool(name="psum", bufs=4))
-        ctx.enter_context(tc.manual_schedule())
 
         def kt(name, shape, dtype):
             return keep.tile(shape, dtype, name=name, align_bytes=64)
@@ -356,13 +355,15 @@ def tile_adversarialsdfconditionalpricingmoments_x2_kernel(
                 )
 
 
-        dummy(6)
+        dummy(7)
         for j in (0, 2):
             for h in range(2):
                 zT(0, h, j, j + 2)
                 zE(0, h, j, j + 2, "SV"[h])
             for h in range(2):
                 zQ(0, h, 128 * j, 128 * (j + 2))
+            if j == 2:
+                dummy(2)
         om = [(j, nh) for j in range(4) for nh in range(2)]
         for k in range(8):
             omM(0, *om[k])
@@ -370,114 +371,126 @@ def tile_adversarialsdfconditionalpricingmoments_x2_kernel(
             if k == 3:
                 bgT()
                 uB()
-        sd(0)
-        for j in range(4):
-            dS(0, j)
         for q in range(4):
             wgM(0, q)
             tanh(0, q)
-            fU(0, q, "G")
+        sd(0)
+        fU(0, 0)
+        fU(0, 1)
+        for j in range(4):
+            dS(0, j)
         for j in (0, 2):
             for h in range(2):
                 zT(1, h, j, j + 2)
                 zE(1, h, j, j + 2, "S")
             for h in range(2):
                 zQ(1, h, 128 * j, 128 * (j + 2))
+        fU(0, 2)
+        fU(0, 3)
         for k in range(4):
             for i in (2 * k, 2 * k + 1):
                 omM(1, *om[i])
                 omR(1, *om[i])
             wgM(1, k)
             tanh(1, k)
-            fU(1, k, "G")
+            if k:
+                fU(1, k - 1)
             dI(0, 256 * k, 256 * (k + 1))
-            if k == 2:
+            if k == 1:
                 fT(0, 0)
                 fT(0, 1)
-                fE(0, 0, "V")
+                fE(0, 0)
                 fE(0, 1)
         sd(1)
+        fU(1, 3)
         for j in range(4):
             dS(1, j)
-        for q in range(4, 8):
+        for q in range(4, 6):
             wgM(0, q)
             tanh(0, q)
-            fU(0, q, "G")
-        dI(1, 0, 256, "V")
-        fQ(0, 0)
-        dI(1, 256, 512, "V")
-        dQ(0, 0, 512)
-        dQ(1, 0, 512)
+        dI(1, 0, 256)
         fT(1, 0)
         fT(1, 1)
-        fE(1, 0)
+        dI(1, 256, 512, "V")
+        fE(1, 0, "V")
         fE(1, 1)
+        fQ(0, 0)
+        dQ(0, 0, 512)
+        dQ(1, 256, 512)
+        dQ(1, 0, 256)
+        fQ(1, 0)
+        for q in range(6, 8):
+            wgM(0, q)
+            tanh(0, q)
+        dI(1, 512, 768)
         for q in range(4, 6):
             wgM(1, q)
             tanh(1, q)
-            fU(1, q, "G")
-        dI(1, 512, 768)
-        fQ(1, 0)
-        dI(1, 768, 1024, "V")
-        dQ(0, 512, 1024)
+        for q in range(4, 8):
+            fU(0, q)
         for it in range(4):
             outM(0, it)
-            outE(0, it, "VS"[it % 2])
+            outE(0, it, "S")
+        dQ(0, 512, 1024)
+        dI(1, 768, 1024, "V")
+        dQ(1, 512, 1024)
         for q in range(6, 8):
             wgM(1, q)
             tanh(1, q)
-            fU(1, q, "GV"[q % 2])
-        dQ(1, 512, 1024)
         fT(0, 2)
         fT(0, 3)
         fE(0, 2, "V")
-        fE(0, 3, "V")
+        fE(0, 3)
+        for q in range(4, 8):
+            fU(1, q)
         for it in range(4, 8):
             outM(0, it)
             outE(0, it, "S")
-        fQ(0, 1)
         for it in range(4):
-            pB(0, it, "GV"[it % 2])
+            pB(0, it, "G")
+        fQ(0, 1)
         fT(1, 2)
         fT(1, 3)
         fE(1, 2, "V")
-        fE(1, 3, "V")
+        fE(1, 3)
         fQ(1, 1)
         for ip in range(2):
             pT(0, ip)
-            pE(0, ip, "V")
+            pE(0, ip, "S")
+        for it in range(4, 8):
+            pB(0, it, "G")
         for it in range(4):
             outM(1, it)
             outE(1, it, "S")
-        for it in range(4, 8):
-            pB(0, it, "GV"[it % 2])
-        for ip in range(2, 4):
-            pT(0, ip)
-            pE(0, ip, "V")
         pQ(0, 0, 512)
         pW(0, 0, 512)
-        for it in range(4):
-            pB(1, it, "GV"[it % 2])
-        for it in range(4, 6):
-            outM(1, it)
-            outE(1, it, "S")
+        for ip in range(2, 4):
+            pT(0, ip)
+            pE(0, ip, "SV"[ip % 2])
         pQ(0, 512, 1024)
         pW(0, 512, 1024)
         pS(0)
+        for it in range(4):
+            pB(1, it, "GV"[it % 2])
         for it in range(6, 8):
             pM(1, it)
-            pD(1, it, "VS"[it % 2])
+            pD(1, it, "SV"[it % 2])
         for it in range(4, 6):
+            outM(1, it)
+            outE(1, it, "S")
             pB(1, it, "V")
-        for ip in range(3):
-            pT(1, ip)
-            pE(1, ip, "VSV"[ip])
         pQ(1, 768, 1024)
+        for ip in range(2):
+            pT(1, ip)
+            pE(1, ip, "VS"[ip])
+        pQ(1, 0, 512)
+        pW(1, 0, 512)
         for it in range(6, 8):
             outM(1, it)
             outE(1, it, "S")
-        pQ(1, 0, 512)
-        pW(1, 0, 512)
+            if it == 6:
+                pT(1, 2)
+                pE(1, 2, "V")
         pQ(1, 512, 768)
         pW(1, 512, 1024)
         pS(1)

@@ -14,8 +14,15 @@ ADD = mybir.AluOpType.add
 MULT = mybir.AluOpType.mult
 ACT = mybir.ActivationFunctionType
 
-T, D, N, Q = 1024, 1024, 1024, 1024
-FLOPS = 3 * 2 * 1024 * 1024 * 1024
+P = 128
+PACK = 4
+PASS = P * PACK
+SIZE = 1024
+HALVES = SIZE // PASS
+BANK = 512
+ROOT = 1.0 / 32.0
+
+FLOPS = 3 * 2 * SIZE * SIZE * SIZE
 
 
 def tile_adversarialsdfconditionalpricingmoments_x2_kernel(
@@ -24,473 +31,440 @@ def tile_adversarialsdfconditionalpricingmoments_x2_kernel(
     nc = tc.nc
     with ExitStack() as ctx:
         keep = ctx.enter_context(tc.tile_pool(name="keep", bufs=1))
-        work = ctx.enter_context(tc.tile_pool(name="work", bufs=4))
+        work = ctx.enter_context(tc.tile_pool(name="work", bufs=8))
         psum = ctx.enter_context(tc.psum_pool(name="psum", bufs=4))
 
-        def kt(name, shape, dtype):
+        def kept(name, shape, dtype):
             return keep.tile(shape, dtype, name=name, align_bytes=64)
 
-        ident = kt("ident", [128, 128], F32)
-        z_sb = [kt("z%d" % g, [128, 4, D], BF16) for g in range(2)]
-        r_sb = [kt("r%d" % g, [128, 4, N], BF16) for g in range(2)]
-        w_sb = {k: kt("w" + k, [128, 2, 2 * N], U8) for k in "og"}
-        ws_sb = {k: kt("ws" + k, [128, 2, N], U8) for k in "og"}
-        bg_rows = kt("bg_rows", [128, 128], BF16)
-        bg_t = kt("bg_t", [128, 8], F32)
-        v_sb = kt("v", [128, 2, 4], BF16)
-        u_row = kt("u_row", [128, T], BF16)
-        ones = kt("ones", [128, 128], BF16)
-        u_bc = kt("u_bc", [128, 2, 512], F32)
-        eye = kt("eye", [128, 8], BF16)
-        warm = kt("warm", [128, 1], F32)
-        zero = kt("zero", [128, 512], BF16)
-        zin = [[kt("zin%d%d" % (g, h), [128, 512, 4], BF16) for h in range(2)] for g in range(2)]
-        zc = [[kt("zc%d%d" % (g, h), [128, 512], U32) for h in range(2)] for g in range(2)]
-        zs = [[kt("zs%d%d" % (g, h), [128, 512], U8) for h in range(2)] for g in range(2)]
-        fin = [kt("fin%d" % g, [128, Q, 4], BF16) for g in range(2)]
-        fc = [kt("fc%d" % g, [128, Q], U32) for g in range(2)]
-        fs = [kt("fs%d" % g, [128, Q], U8) for g in range(2)]
-        dsc = [kt("dsc%d" % g, [128, 4, N], BF16) for g in range(2)]
-        din = [kt("din%d" % g, [128, N, 4], BF16) for g in range(2)]
-        dc = [kt("dc%d" % g, [128, N], U32) for g in range(2)]
-        ds = [kt("ds%d" % g, [128, N], U8) for g in range(2)]
-        acc = [kt("acc%d" % g, [128, 4, 2], F32) for g in range(2)]
-        sv = [kt("sv%d" % g, [128, 3, 4], F32) for g in range(2)]
-        pin = [kt("pin%d" % h, [128, N, 4], BF16) for h in range(2)]
-        pc = [kt("pc%d" % h, [128, N], U32) for h in range(2)]
-        ps = [kt("ps%d" % h, [128, N], U8) for h in range(2)]
+        def kept_pair(name, shape, dtype):
+            return [kept("%s_%d" % (name, i), shape, dtype) for i in range(HALVES)]
 
-        nc.vector.memset(zero[:], 0.0)
-        for k in "og":
-            nc.vector.memset(ws_sb[k][:].rearrange("p g n -> p (g n)").bitcast(I32), 0)
-        nc.vector.memset(bg_rows[:], 0.0)
-        nc.vector.memset(warm[:], 0.0)
-        nc.vector.memset(u_row[:], 0.0)
-        nc.vector.memset(ones[:], 1.0)
-        nc.scalar.activation(out=warm[:], in_=warm[:], func=ACT.Tanh)
+        identity = kept("identity", [P, P], F32)
+        identity_8 = kept("identity_8", [P, 8], BF16)
+        ones = kept("ones", [P, P], BF16)
+        zero = kept("zero", [P, 1], F32)
+        z_rows = kept_pair("z_rows", [P, PACK, SIZE], BF16)
+        r_rows = kept_pair("r_rows", [P, PACK, SIZE], BF16)
+        wo_codes = kept("wo_codes", [P, HALVES, 2 * SIZE], U8)
+        wg_codes = kept("wg_codes", [P, HALVES, 2 * SIZE], U8)
+        wo_bytes = kept("wo_bytes", [P, HALVES, SIZE], U8)
+        wg_bytes = kept("wg_bytes", [P, HALVES, SIZE], U8)
+        bg_rows = kept("bg_rows", [P, P], BF16)
+        bg_col = kept("bg_col", [P, 8], F32)
+        u_row = kept("u_row", [P, SIZE], BF16)
+        u_all = kept("u_all", [P, HALVES, PASS], F32)
+        v_col = kept("v_col", [P, HALVES, PACK], BF16)
+        z_in = [kept_pair("z_in_%d" % g, [P, PASS, PACK], BF16) for g in range(HALVES)]
+        z_codes = [kept_pair("z_codes_%d" % g, [P, PASS], U32) for g in range(HALVES)]
+        z_bytes = [kept_pair("z_bytes_%d" % g, [P, PASS], U8) for g in range(HALVES)]
+        f_in = kept_pair("f_in", [P, SIZE, PACK], BF16)
+        f_codes = kept_pair("f_codes", [P, SIZE], U32)
+        f_bytes = kept_pair("f_bytes", [P, SIZE], U8)
+        returns = kept_pair("returns", [P, PACK, HALVES], F32)
+        sdf_parts = kept_pair("sdf_parts", [P, 3, PACK], F32)
+        d_rows = kept_pair("d_rows", [P, PACK, SIZE], BF16)
+        d_in = kept_pair("d_in", [P, SIZE, PACK], BF16)
+        d_codes = kept_pair("d_codes", [P, SIZE], U32)
+        d_bytes = kept_pair("d_bytes", [P, SIZE], U8)
+        y_in = kept_pair("y_in", [P, SIZE, PACK], BF16)
+        y_codes = kept_pair("y_codes", [P, SIZE], U32)
+        y_bytes = kept_pair("y_bytes", [P, SIZE], U8)
 
-        def load_z(g, j0, j1):
-            nc.sync.dma_start(
-                out=z_sb[g][:, j0:j1, :],
-                in_=z[512 * g : 512 * (g + 1), :].rearrange("(p j) d -> p j d", j=4)[:, j0:j1, :],
+        def product_bank():
+            return psum.tile([P, BANK], F32, name="product")
+
+        def turn_bank(shape):
+            return psum.tile(shape, F32, name="turn")
+
+        def flat(ap):
+            return ap.rearrange("p c k -> p (c k)")
+
+        def words(ap):
+            return flat(ap).bitcast(F32).rearrange("p (c e) -> p c e", e=2)
+
+        def quantise(codes, scale_bytes, values, cols):
+            nc.vector.quantize_mx(
+                out=codes[:, cols].bitcast(E4M3), scales=scale_bytes[:, cols], in_=flat(values[:, cols, :])
             )
 
-        def load_scales(eng, k, src):
+        def copy_on(engine, out, in_):
+            if engine == "S":
+                nc.scalar.copy(out=out, in_=in_)
+            else:
+                nc.vector.tensor_copy(out=out, in_=in_)
+
+        for scale_tile in (wo_bytes, wg_bytes):
+            nc.vector.memset(flat(scale_tile[:]).bitcast(I32), 0)
+        nc.vector.memset(u_row[:], 0.0)
+        nc.vector.memset(bg_rows[:], 0.0)
+        nc.vector.memset(ones[:], 1.0)
+        nc.vector.memset(zero[:], 0.0)
+        nc.scalar.activation(out=zero[:], in_=zero[:], func=ACT.Tanh)
+
+        def load_rows(tile, src, g, j):
+            rows = src[PASS * g : PASS * (g + 1), :].rearrange("(p j) n -> p j n", j=PACK)
+            nc.sync.dma_start(out=tile[g][:, j : j + 2, :], in_=rows[:, j : j + 2, :])
+
+        def load_words(tile, src):
+            nc.sync.dma_start(out=tile[:].bitcast(I32), in_=src.rearrange("g p n -> p g n").bitcast(I32))
+
+        def load_scales(queue, tile, src):
             for b in range(4):
-                eng.dma_start(
-                    out=ws_sb[k][32 * b : 32 * b + 4, :, :].bitcast(I32),
+                queue.dma_start(
+                    out=tile[32 * b : 32 * b + 4, :, :].bitcast(I32),
                     in_=src[:, 4 * b : 4 * b + 4, :].rearrange("g q n -> q g n").bitcast(I32),
                 )
 
-        def load_words(k, src, c0, c1):
-            nc.sync.dma_start(
-                out=w_sb[k][:, :, c0:c1].bitcast(I32), in_=src.rearrange("g p n -> p g n")[:, :, c0:c1].bitcast(I32)
-            )
-
-        def load_r(g, j0, j1):
-            nc.sync.dma_start(
-                out=r_sb[g][:, j0:j1, :],
-                in_=r[512 * g : 512 * (g + 1), :].rearrange("(p j) i -> p j i", j=4)[:, j0:j1, :],
-            )
-
-        load_z(0, 0, 2)
-        load_z(0, 2, 4)
-        load_scales(nc.scalar, "o", wo_scales)
-        load_words("o", wo_words, 0, 2 * N)
-        load_r(0, 0, 2)
-        load_r(0, 2, 4)
-        load_words("g", wg_words, 0, 2 * N)
-        load_z(1, 0, 4)
-        load_r(1, 0, 4)
-        make_identity(nc, ident[:])
-        nc.gpsimd.dma_start(out=bg_rows[0:8, :], in_=bg.rearrange("(a p) -> a p", p=128))
-        nc.gpsimd.dma_start(out=v_sb[:], in_=v.rearrange("(g p j) -> p g j", p=128, j=4))
+        load_rows(z_rows, z, 0, 0)
+        load_rows(z_rows, z, 0, 2)
+        load_scales(nc.scalar, wo_bytes, wo_scales)
+        load_words(wo_codes, wo_words)
+        load_rows(r_rows, r, 0, 0)
+        load_rows(r_rows, r, 0, 2)
+        load_rows(z_rows, z, 1, 0)
+        load_rows(z_rows, z, 1, 2)
+        load_words(wg_codes, wg_words)
+        load_rows(r_rows, r, 1, 0)
+        load_rows(r_rows, r, 1, 2)
+        make_identity(nc, identity[:])
+        nc.gpsimd.dma_start(out=bg_rows[0:8, :], in_=bg.rearrange("(a p) -> a p", p=P))
+        nc.gpsimd.dma_start(out=v_col[:], in_=v.rearrange("(g p j) -> p g j", p=P, j=PACK))
         nc.gpsimd.dma_start(out=u_row[0:1, :], in_=u.unsqueeze(0))
-        load_scales(nc.gpsimd, "g", wg_scales)
+        load_scales(nc.gpsimd, wg_bytes, wg_scales)
 
-        def bank(tag, shape):
-            return psum.tile(shape, F32, name=tag, tag=tag)
+        live = {}
 
-        hold = {}
+        def bias_columns():
+            nc.scalar.copy(out=identity_8[:], in_=identity[:, 0:8])
+            bank = turn_bank([P, 8])
+            nc.tensor.matmul(bank[:], bg_rows[:], identity_8[:], start=True, stop=True)
+            nc.scalar.activation(out=bg_col[:], in_=bank[:], func=ACT.Identity, bias=zero[:])
 
-        def zT(g, h, j0, j1):
-            n = 128 * (j1 - j0)
-            t = bank("tr", [128, 2, n])
-            w = z_sb[g][:].rearrange("p j d -> p (j d)").bitcast(F32).rearrange("p (j w) -> p j w", j=4)
-            for j in range(j0, j1):
-                for e in range(2):
-                    nc.tensor.transpose(
-                        t[:, e, 128 * (j - j0) : 128 * (j - j0 + 1)], w[:, j, 256 * h + e : 256 * (h + 1) : 2], ident[:]
-                    )
-            hold["z", g, h, j0] = t
-
-        def zE(g, h, j0, j1, eng):
-            o = zin[g][h][:, 128 * j0 : 128 * j1, :].rearrange("p c k -> p (c k)").bitcast(F32).rearrange("p (c e) -> p c e", e=2)
-            i = hold["z", g, h, j0][:].rearrange("p e c -> p c e")
-            if eng == "S":
-                nc.scalar.copy(out=o, in_=i)
-            else:
-                nc.vector.tensor_copy(out=o, in_=i)
-
-        def dummy(n):
-            for k in range(n):
-                t = bank("mm", [128, 512])
-                nc.tensor.matmul(t[:], zero[:, 0:128], zero[:], start=True, stop=True)
-
-        def zQ(g, h, c0, c1):
-            nc.vector.quantize_mx(
-                out=zc[g][h][:, c0:c1].bitcast(E4M3),
-                scales=zs[g][h][:, c0:c1],
-                in_=zin[g][h][:, c0:c1, :].rearrange("p c k -> p (c k)"),
-            )
-
-        def bgT():
-            nc.scalar.copy(out=eye[:], in_=ident[:, 0:8])
-            t = bank("tr", [128, 8])
-            nc.tensor.matmul(t[:], bg_rows[:], eye[:], start=True, stop=True)
-            nc.scalar.copy(out=bg_t[:], in_=t[:])
-
-        def wgM(g, qt):
-            t = bank("mm", [128, 512])
-            for h in range(2):
-                nc.tensor.matmul_mx(
-                    out=t[:],
-                    lhsT=w_sb["g"][:, h, 256 * qt : 256 * (qt + 1)].bitcast(E2M1),
-                    lhsT_scale=ws_sb["g"][:, h, 128 * qt : 128 * (qt + 1)],
-                    rhs=zc[g][h][:].bitcast(E4M3),
-                    rhs_scale=zs[g][h][:],
-                    start=h == 0,
-                    stop=h == 1,
-                )
-            hold["x", g, qt] = t
-
-        def tanh(g, qt):
-            t = work.tile([128, 512], F32, name="th", bufs=12)
-            nc.scalar.activation(out=t[:], in_=hold["x", g, qt][:], func=ACT.Tanh, bias=bg_t[:, qt : qt + 1])
-            hold["t", g, qt] = t
-
-        def uB():
-            for g in range(2):
-                t = bank("tr", [128, 512])
-                nc.tensor.matmul(t[:], ones[:], u_row[:, 512 * g : 512 * (g + 1)], start=True, stop=True)
+        def weights_on_all_partitions():
+            for g in range(HALVES):
+                bank = turn_bank([P, PASS])
+                nc.tensor.matmul(bank[:], ones[:], u_row[:, PASS * g : PASS * (g + 1)], start=True, stop=True)
                 nc.scalar.copy(
-                    out=u_bc[:, g, :].rearrange("p (w c e) -> p w c e", w=2, e=2),
-                    in_=t[:].rearrange("p (c w e) -> p w c e", w=2, e=2),
+                    out=u_all[:, g, :].rearrange("p (w c e) -> p w c e", w=2, e=2),
+                    in_=bank[:].rearrange("p (c w e) -> p w c e", w=2, e=2),
                 )
 
-        def fU(g, qt, eng="V"):
-            t = work.tile([128, 512], BF16, name="fb", bufs=8)
-            (nc.vector if eng == "V" else nc.gpsimd).tensor_tensor(
-                out=t[:].rearrange("p (w c e) -> p w c e", w=2, e=2),
-                in0=hold["t", g, qt][:].rearrange("p (w e c) -> p w c e", w=2, e=2),
-                in1=u_bc[:, g, :].rearrange("p (w c e) -> p w c e", w=2, e=2),
-                op=MULT,
-            )
-            hold["b", g, qt] = t
+        def z_turn(g, c, j):
+            bank = turn_bank([P, 2, 2 * P])
+            z_words = flat(z_rows[g][:]).bitcast(F32).rearrange("p (j w) -> p j w", j=PACK)
+            for i in range(2):
+                for w in range(2):
+                    nc.tensor.transpose(
+                        bank[:, w, P * i : P * (i + 1)],
+                        z_words[:, j + i, 2 * P * c + w : 2 * P * (c + 1) : 2],
+                        identity[:],
+                    )
+            live["z", g, c, j] = bank
 
-        def fT(g, qp):
-            t = bank("tr", [128, 2, 256])
-            for k in range(2):
-                w = hold["b", g, 2 * qp + k][:].bitcast(F32)
-                for e in range(2):
-                    nc.tensor.transpose(t[:, e, 128 * k : 128 * (k + 1)], w[:, 128 * e : 128 * (e + 1)], ident[:])
-            hold["f", g, qp] = t
+        def z_take(g, c, j, engine):
+            cols = slice(P * j, P * (j + 2))
+            copy_on(engine, words(z_in[g][c][:, cols, :]), live["z", g, c, j][:].rearrange("p w n -> p n w"))
 
-        def fE(g, qp, eng="S"):
-            w = fin[g][:].rearrange("p c k -> p (c k)").bitcast(F32).rearrange("p (h j b a e) -> p h j b a e", h=2, j=4, b=2, a=64)
-            o = w[:, qp // 2, :, qp % 2, :, :]
-            i = hold["f", g, qp][:].rearrange("p e (a j) -> p j a e", j=4)
-            if eng == "S":
-                nc.scalar.copy(out=o, in_=i)
-            else:
-                nc.vector.tensor_copy(out=o, in_=i)
+        def z_quantise(g, c, j):
+            quantise(z_codes[g][c], z_bytes[g][c], z_in[g][c], slice(P * j, P * (j + 2)))
 
-        def fQ(g, h):
-            c = slice(512 * h, 512 * (h + 1))
-            nc.vector.quantize_mx(
-                out=fc[g][:, c].bitcast(E4M3), scales=fs[g][:, c], in_=fin[g][:, c, :].rearrange("p c k -> p (c k)")
-            )
-
-        def omM(g, j, nh):
-            t = bank("mm", [128, 512])
-            for h in range(2):
+        def om_product(g, j, n):
+            bank = product_bank()
+            cols = slice(P * j, P * (j + 1))
+            for c in range(HALVES):
                 nc.tensor.matmul_mx(
-                    out=t[:],
-                    lhsT=zc[g][h][:, 128 * j : 128 * (j + 1)].bitcast(E4M3),
-                    lhsT_scale=zs[g][h][:, 128 * j : 128 * (j + 1)],
-                    rhs=w_sb["o"][:, h, 1024 * nh : 1024 * (nh + 1)].bitcast(E2M1),
-                    rhs_scale=ws_sb["o"][:, h, 512 * nh : 512 * (nh + 1)],
-                    start=h == 0,
-                    stop=h == 1,
+                    out=bank[:],
+                    lhsT=z_codes[g][c][:, cols].bitcast(E4M3),
+                    lhsT_scale=z_bytes[g][c][:, cols],
+                    rhs=wo_codes[:, c, 2 * BANK * n : 2 * BANK * (n + 1)].bitcast(E2M1),
+                    rhs_scale=wo_bytes[:, c, BANK * n : BANK * (n + 1)],
+                    start=c == 0,
+                    stop=c == HALVES - 1,
                 )
-            hold["o", g, j, nh] = t
+            live["om", g, j, n] = bank
 
-        def omR(g, j, nh):
-            junk = work.tile([128, 512], F32, name="junk", bufs=2)
+        def om_return(g, j, n):
+            om_r = work.tile([P, BANK], F32, name="om_r", bufs=2)
             nc.vector.scalar_tensor_tensor(
-                out=junk[:],
-                in0=hold["o", g, j, nh][:],
+                out=om_r[:],
+                in0=live["om", g, j, n][:],
                 scalar=1.0,
-                in1=r_sb[g][:, j, 512 * nh : 512 * (nh + 1)],
+                in1=r_rows[g][:, j, BANK * n : BANK * (n + 1)],
                 op0=MULT,
                 op1=MULT,
-                accum_out=acc[g][:, j, nh : nh + 1],
+                accum_out=returns[g][:, j, n : n + 1],
             )
 
-        def sd(g):
-            a, b, c = (sv[g][:, k, :] for k in range(3))
-            nc.vector.tensor_tensor(out=a, in0=acc[g][:, :, 0], in1=acc[g][:, :, 1], op=ADD)
-            nc.vector.tensor_scalar(out=b, in0=a, scalar1=-1.0 / 32, scalar2=1.0, op0=MULT, op1=ADD)
-            nc.vector.tensor_tensor(out=c, in0=b, in1=v_sb[:, g, :], op=MULT)
+        def sdf_weight(g):
+            total, sdf, v_sdf = (sdf_parts[g][:, i, :] for i in range(3))
+            nc.gpsimd.tensor_tensor(out=total, in0=returns[g][:, :, 0], in1=returns[g][:, :, 1], op=ADD)
+            nc.gpsimd.tensor_scalar(out=sdf, in0=total, scalar1=-ROOT, scalar2=1.0, op0=MULT, op1=ADD)
+            nc.gpsimd.tensor_tensor(out=v_sdf, in0=sdf, in1=v_col[:, g, :], op=MULT)
 
-        def dS(g, j, eng="V"):
-            a = dict(out=dsc[g][:, j, :], in0=r_sb[g][:, j, :], scalar1=sv[g][:, 2, j : j + 1], op0=MULT)
-            if eng == "V":
-                nc.vector.tensor_scalar(scalar2=None, **a)
-            else:
-                nc.gpsimd.tensor_scalar(scalar2=0.0, op1=ADD, **a)
+        def d_scale(g):
+            for j in range(PACK):
+                nc.vector.tensor_scalar(
+                    out=d_rows[g][:, j, :],
+                    in0=r_rows[g][:, j, :],
+                    scalar1=sdf_parts[g][:, 2, j : j + 1],
+                    scalar2=None,
+                    op0=MULT,
+                )
 
-        def dI(g, c0, c1, eng="S"):
-            o, i = din[g][:, c0:c1, :], dsc[g][:, :, c0:c1].rearrange("p j c -> p c j")
-            if eng == "S":
-                nc.scalar.copy(out=o, in_=i)
-            else:
-                nc.vector.tensor_copy(out=o, in_=i)
+        def d_interleave(g, quarter, engine):
+            cols = slice(2 * P * quarter, 2 * P * (quarter + 1))
+            copy_on(engine, d_in[g][:, cols, :], d_rows[g][:, :, cols].rearrange("p j n -> p n j"))
 
-        def dQ(g, c0, c1):
-            nc.vector.quantize_mx(
-                out=dc[g][:, c0:c1].bitcast(E4M3), scales=ds[g][:, c0:c1], in_=din[g][:, c0:c1, :].rearrange("p c k -> p (c k)")
-            )
+        def d_quantise(g, a0, a1):
+            quantise(d_codes[g], d_bytes[g], d_in[g], slice(a0, a1))
 
-        def outM(h, it):
-            t = bank("mm", [128, 512])
-            for g in range(2):
+        def x_product(g, a):
+            bank = product_bank()
+            for c in range(HALVES):
                 nc.tensor.matmul_mx(
-                    out=t[:],
-                    lhsT=dc[g][:, 128 * it : 128 * (it + 1)].bitcast(E4M3),
-                    lhsT_scale=ds[g][:, 128 * it : 128 * (it + 1)],
-                    rhs=fc[g][:, 512 * h : 512 * (h + 1)].bitcast(E4M3),
-                    rhs_scale=fs[g][:, 512 * h : 512 * (h + 1)],
+                    out=bank[:],
+                    lhsT=wg_codes[:, c, 2 * P * a : 2 * P * (a + 1)].bitcast(E2M1),
+                    lhsT_scale=wg_bytes[:, c, P * a : P * (a + 1)],
+                    rhs=z_codes[g][c][:].bitcast(E4M3),
+                    rhs_scale=z_bytes[g][c][:],
+                    start=c == 0,
+                    stop=c == HALVES - 1,
+                )
+            tanh_x = work.tile([P, PASS], F32, name="tanh_x", bufs=12)
+            nc.scalar.activation(out=tanh_x[:], in_=bank[:], func=ACT.Tanh, bias=bg_col[:, a : a + 1])
+            live["tanh", g, a] = tanh_x
+
+        def f_scale(g, a):
+            f_t = work.tile([P, PASS], BF16, name="f_t")
+            nc.vector.tensor_tensor(
+                out=f_t[:].rearrange("q (w p e) -> q w p e", w=2, e=2),
+                in0=live["tanh", g, a][:].rearrange("q (w e p) -> q w p e", w=2, e=2),
+                in1=u_all[:, g, :].rearrange("q (w p e) -> q w p e", w=2, e=2),
+                op=MULT,
+            )
+            live["f", g, a] = f_t
+
+        def words_turn(first, second):
+            bank = turn_bank([P, 2, 2 * P])
+            for i, tile in enumerate((first, second)):
+                pairs = tile[:].bitcast(F32)
+                for w in range(2):
+                    nc.tensor.transpose(bank[:, w, P * i : P * (i + 1)], pairs[:, P * w : P * (w + 1)], identity[:])
+            return bank
+
+        def f_turn(g, pair):
+            live["f turned", g, pair] = words_turn(live["f", g, 2 * pair], live["f", g, 2 * pair + 1])
+
+        def f_take(g, pair, engine):
+            cols = words(f_in[g][:]).rearrange("p (h j m b) w -> p h m j b w", h=2, j=PACK, m=2)
+            bank = live["f turned", g, pair][:].rearrange("p w (b j) -> p j b w", j=PACK)
+            copy_on(engine, cols[:, pair // 2, pair % 2, :, :, :], bank)
+
+        def f_quantise(g, h):
+            quantise(f_codes[g], f_bytes[g], f_in[g], slice(PASS * h, PASS * (h + 1)))
+
+        def out_product(h, a):
+            bank = product_bank()
+            rows, cols = slice(P * a, P * (a + 1)), slice(PASS * h, PASS * (h + 1))
+            for g in range(HALVES):
+                nc.tensor.matmul_mx(
+                    out=bank[:],
+                    lhsT=d_codes[g][:, rows].bitcast(E4M3),
+                    lhsT_scale=d_bytes[g][:, rows],
+                    rhs=f_codes[g][:, cols].bitcast(E4M3),
+                    rhs_scale=f_bytes[g][:, cols],
                     start=g == 0,
-                    stop=g == 1,
+                    stop=g == HALVES - 1,
                 )
-            hold["out", h, it] = t
+            y = work.tile([P, PASS], F32, name="y")
+            nc.scalar.mul(
+                out=y[:].rearrange("i (p j) -> i p j", j=PACK),
+                in_=bank[:].rearrange("i (j p) -> i p j", j=PACK),
+                mul=ROOT,
+            )
+            nc.sync.dma_start(out=out_0[rows, cols], in_=y[:])
+            live["y", h, a] = y
 
-        def outE(h, it, eng="S"):
-            t = work.tile([128, 512], F32, name="osb", bufs=8)
-            o = t[:].rearrange("p (c j) -> p c j", j=4)
-            i = hold["out", h, it][:].rearrange("p (j c) -> p c j", j=4)
-            if eng == "S":
-                nc.scalar.mul(out=o, in_=i, mul=1.0 / 32)
+        def y_round(h, a, engine):
+            y_t = work.tile([P, PASS], BF16, name="y_t")
+            rounded = y_t[:].rearrange("i (w p e) -> i w p e", w=2, e=2)
+            exact = live["y", h, a][:].rearrange("i (p w e) -> i w p e", w=2, e=2)
+            if engine == "G":
+                nc.gpsimd.tensor_scalar(out=rounded, in0=exact, scalar1=1.0, scalar2=0.0, op0=MULT, op1=ADD)
             else:
-                nc.vector.tensor_scalar(out=o, in0=i, scalar1=1.0 / 32, scalar2=None, op0=MULT)
-            nc.sync.dma_start(out=out_0[128 * it : 128 * (it + 1), 512 * h : 512 * (h + 1)], in_=t[:])
-            hold["os", h, it] = t
+                nc.vector.tensor_copy(out=rounded, in_=exact)
+            live["y rounded", h, a] = y_t
 
-        def pB(h, it, eng="V"):
-            t = work.tile([128, 512], BF16, name="ob", bufs=8)
-            o = t[:].rearrange("p (w c e) -> p w c e", w=2, e=2)
-            i = hold["os", h, it][:].rearrange("p (c w e) -> p w c e", w=2, e=2)
-            if eng == "V":
-                nc.vector.tensor_copy(out=o, in_=i)
-            else:
-                nc.gpsimd.tensor_scalar(out=o, in0=i, scalar1=1.0, scalar2=0.0, op0=MULT, op1=ADD)
-            hold["ob", h, it] = t
+        def y_turn(h, pair):
+            live["y turned", h, pair] = words_turn(
+                live["y rounded", h, 2 * pair], live["y rounded", h, 2 * pair + 1]
+            )
 
-        def pT(h, ip):
-            t = bank("tr", [128, 2, 256])
-            for k in range(2):
-                w = hold["ob", h, 2 * ip + k][:].bitcast(F32)
-                for e in range(2):
-                    nc.tensor.transpose(t[:, e, 128 * k : 128 * (k + 1)], w[:, 128 * e : 128 * (e + 1)], ident[:])
-            hold["pt", h, ip] = t
+        def y_take(h, pair, engine):
+            cols = slice(2 * P * pair, 2 * P * (pair + 1))
+            copy_on(engine, words(y_in[h][:, cols, :]), live["y turned", h, pair][:].rearrange("p w n -> p n w"))
 
-        def pE(h, ip, eng):
-            c = slice(256 * ip, 256 * (ip + 1))
-            o = pin[h][:, c, :].rearrange("p c k -> p (c k)").bitcast(F32).rearrange("p (c e) -> p c e", e=2)
-            i = hold["pt", h, ip][:].rearrange("p e c -> p c e")
-            if eng == "S":
-                nc.scalar.copy(out=o, in_=i)
-            else:
-                nc.vector.tensor_copy(out=o, in_=i)
-
-        def pM(h, it):
-            t = bank("tr", [128, 4, 128])
-            for j in range(4):
-                c = slice(512 * h + 128 * j, 512 * h + 128 * (j + 1))
-                for g in range(2):
+        def y_direct_product(h, a):
+            bank = turn_bank([P, PACK, P])
+            rows = slice(P * a, P * (a + 1))
+            for j in range(PACK):
+                cols = slice(PASS * h + P * j, PASS * h + P * (j + 1))
+                for g in range(HALVES):
                     nc.tensor.matmul_mx(
-                        out=t[:, j, :],
-                        lhsT=fc[g][:, c].bitcast(E4M3),
-                        lhsT_scale=fs[g][:, c],
-                        rhs=dc[g][:, 128 * it : 128 * (it + 1)].bitcast(E4M3),
-                        rhs_scale=ds[g][:, 128 * it : 128 * (it + 1)],
+                        out=bank[:, j, :],
+                        lhsT=f_codes[g][:, cols].bitcast(E4M3),
+                        lhsT_scale=f_bytes[g][:, cols],
+                        rhs=d_codes[g][:, rows].bitcast(E4M3),
+                        rhs_scale=d_bytes[g][:, rows],
                         start=g == 0,
-                        stop=g == 1,
+                        stop=g == HALVES - 1,
                     )
-            hold["pm", h, it] = t
+            live["y direct", h, a] = bank
 
-        def pD(h, it, eng):
-            o = pin[h][:, 128 * it : 128 * (it + 1), :]
-            i = hold["pm", h, it][:].rearrange("p j c -> p c j")
-            if eng == "S":
-                nc.scalar.mul(out=o, in_=i, mul=1.0 / 32)
+        def y_direct_take(h, a, engine):
+            out = y_in[h][:, P * a : P * (a + 1), :]
+            bank = live["y direct", h, a][:].rearrange("p j n -> p n j")
+            if engine == "S":
+                nc.scalar.mul(out=out, in_=bank, mul=ROOT)
             else:
-                nc.vector.tensor_scalar(out=o, in0=i, scalar1=1.0 / 32, scalar2=None, op0=MULT)
+                nc.vector.tensor_scalar(out=out, in0=bank, scalar1=ROOT, scalar2=None, op0=MULT)
 
-        def pQ(h, c0, c1):
-            nc.vector.quantize_mx(
-                out=pc[h][:, c0:c1].bitcast(E4M3), scales=ps[h][:, c0:c1], in_=pin[h][:, c0:c1, :].rearrange("p c k -> p (c k)")
-            )
+        def y_quantise(h, a0, a1):
+            quantise(y_codes[h], y_bytes[h], y_in[h], slice(a0, a1))
 
-        def pW(h, c0, c1):
+        def store_words(h, a0, a1):
             nc.sync.dma_start(
-                out=out_1[h].rearrange("p m t -> p (m t)")[:, 4 * c0 : 4 * c1].bitcast(I32), in_=pc[h][:, c0:c1].bitcast(I32)
+                out=flat(out_1[h])[:, PACK * a0 : PACK * a1].bitcast(I32), in_=y_codes[h][:, a0:a1].bitcast(I32)
             )
 
-        def pS(h, eng=None):
+        def store_scales(h):
             for b in range(4):
-                (eng or nc.sync).dma_start(
-                    out=out_2[h, 4 * b : 4 * b + 4, :].bitcast(I32), in_=ps[h][32 * b : 32 * b + 4, :].bitcast(I32)
+                nc.sync.dma_start(
+                    out=out_2[h, 4 * b : 4 * b + 4, :].bitcast(I32),
+                    in_=y_bytes[h][32 * b : 32 * b + 4, :].bitcast(I32),
                 )
 
+        om_steps = [(j, n) for j in range(PACK) for n in range(HALVES)]
 
-        dummy(7)
-        for j in (0, 2):
-            for h in range(2):
-                zT(0, h, j, j + 2)
-                zE(0, h, j, j + 2, "SV"[h])
-            for h in range(2):
-                zQ(0, h, 128 * j, 128 * (j + 2))
-            if j == 2:
-                dummy(2)
-        om = [(j, nh) for j in range(4) for nh in range(2)]
-        for k in range(8):
-            omM(0, *om[k])
-            omR(0, *om[k])
-            if k == 3:
-                bgT()
-                uB()
-        for q in range(4):
-            wgM(0, q)
-            tanh(0, q)
-        sd(0)
-        fU(0, 0)
-        fU(0, 1)
-        for j in range(4):
-            dS(0, j)
-        for j in (0, 2):
-            for h in range(2):
-                zT(1, h, j, j + 2)
-                zE(1, h, j, j + 2, "S")
-            for h in range(2):
-                zQ(1, h, 128 * j, 128 * (j + 2))
-        fU(0, 2)
-        fU(0, 3)
-        for k in range(4):
-            for i in (2 * k, 2 * k + 1):
-                omM(1, *om[i])
-                omR(1, *om[i])
-            wgM(1, k)
-            tanh(1, k)
-            if k:
-                fU(1, k - 1)
-            dI(0, 256 * k, 256 * (k + 1))
-            if k == 1:
-                fT(0, 0)
-                fT(0, 1)
-                fE(0, 0)
-                fE(0, 1)
-        sd(1)
-        fU(1, 3)
-        for j in range(4):
-            dS(1, j)
-        for q in range(4, 6):
-            wgM(0, q)
-            tanh(0, q)
-        dI(1, 0, 256)
-        fT(1, 0)
-        fT(1, 1)
-        dI(1, 256, 512, "V")
-        fE(1, 0, "V")
-        fE(1, 1)
-        fQ(0, 0)
-        dQ(0, 0, 512)
-        dQ(1, 256, 512)
-        dQ(1, 0, 256)
-        fQ(1, 0)
-        for q in range(6, 8):
-            wgM(0, q)
-            tanh(0, q)
-        dI(1, 512, 768)
-        for q in range(4, 6):
-            wgM(1, q)
-            tanh(1, q)
-        for q in range(4, 8):
-            fU(0, q)
-        for it in range(4):
-            outM(0, it)
-            outE(0, it, "S")
-        dQ(0, 512, 1024)
-        dI(1, 768, 1024, "V")
-        dQ(1, 512, 1024)
-        for q in range(6, 8):
-            wgM(1, q)
-            tanh(1, q)
-        fT(0, 2)
-        fT(0, 3)
-        fE(0, 2, "V")
-        fE(0, 3)
-        for q in range(4, 8):
-            fU(1, q)
-        for it in range(4, 8):
-            outM(0, it)
-            outE(0, it, "S")
-        for it in range(4):
-            pB(0, it, "G")
-        fQ(0, 1)
-        fT(1, 2)
-        fT(1, 3)
-        fE(1, 2, "V")
-        fE(1, 3)
-        fQ(1, 1)
-        for ip in range(2):
-            pT(0, ip)
-            pE(0, ip, "S")
-        for it in range(4, 8):
-            pB(0, it, "G")
-        for it in range(4):
-            outM(1, it)
-            outE(1, it, "S")
-        pQ(0, 0, 512)
-        pW(0, 0, 512)
-        for ip in range(2, 4):
-            pT(0, ip)
-            pE(0, ip, "SV"[ip % 2])
-        pQ(0, 512, 1024)
-        pW(0, 512, 1024)
-        pS(0)
-        for it in range(4):
-            pB(1, it, "GV"[it % 2])
-        for it in range(6, 8):
-            pM(1, it)
-            pD(1, it, "SV"[it % 2])
-        for it in range(4, 6):
-            outM(1, it)
-            outE(1, it, "S")
-            pB(1, it, "V")
-        pQ(1, 768, 1024)
-        for ip in range(2):
-            pT(1, ip)
-            pE(1, ip, "VS"[ip])
-        pQ(1, 0, 512)
-        pW(1, 0, 512)
-        for it in range(6, 8):
-            outM(1, it)
-            outE(1, it, "S")
-            if it == 6:
-                pT(1, 2)
-                pE(1, 2, "V")
-        pQ(1, 512, 768)
-        pW(1, 512, 1024)
-        pS(1)
+        def z_half(g, engines):
+            for j in (0, 2):
+                for c in range(HALVES):
+                    z_turn(g, c, j)
+                    z_take(g, c, j, engines[c])
+                for c in range(HALVES):
+                    z_quantise(g, c, j)
+
+        z_half(0, "SV")
+        for i, step in enumerate(om_steps):
+            om_product(0, *step)
+            om_return(0, *step)
+            if i == 3:
+                bias_columns()
+                weights_on_all_partitions()
+        sdf_weight(0)
+        z_half(1, "SS")
+        d_scale(0)
+
+        for a in range(4):
+            x_product(0, a)
+        for a in range(4):
+            f_scale(0, a)
+        for a in range(4):
+            for step in om_steps[2 * a : 2 * a + 2]:
+                om_product(1, *step)
+                om_return(1, *step)
+            x_product(1, a)
+            if a > 0:
+                f_scale(1, a - 1)
+            d_interleave(0, a, "S")
+            if a == 1:
+                for pair in range(2):
+                    f_turn(0, pair)
+                for pair in range(2):
+                    f_take(0, pair, "S")
+        sdf_weight(1)
+        f_scale(1, 3)
+        d_scale(1)
+
+        for a in range(4, 6):
+            x_product(0, a)
+        d_interleave(1, 0, "S")
+        for pair in range(2):
+            f_turn(1, pair)
+        d_interleave(1, 1, "V")
+        for pair in range(2):
+            f_take(1, pair, "VS"[pair])
+        f_quantise(0, 0)
+        d_quantise(0, 0, 512)
+        d_quantise(1, 256, 512)
+        d_quantise(1, 0, 256)
+        f_quantise(1, 0)
+        for a in range(6, 8):
+            x_product(0, a)
+        for a in range(4, 6):
+            x_product(1, a)
+        d_interleave(1, 2, "S")
+        for a in range(4, 8):
+            f_scale(0, a)
+        for a in range(4):
+            out_product(0, a)
+        d_quantise(0, 512, 1024)
+        d_interleave(1, 3, "V")
+        d_quantise(1, 512, 1024)
+        for a in range(6, 8):
+            x_product(1, a)
+        for pair in range(2, 4):
+            f_turn(0, pair)
+        for pair in range(2, 4):
+            f_take(0, pair, "VS"[pair % 2])
+        for a in range(4, 8):
+            f_scale(1, a)
+        for a in range(4, 8):
+            out_product(0, a)
+        for a in range(4):
+            y_round(0, a, "G")
+        f_quantise(0, 1)
+        for pair in range(2, 4):
+            f_turn(1, pair)
+        for pair in range(2, 4):
+            f_take(1, pair, "VS"[pair % 2])
+        f_quantise(1, 1)
+
+        for pair in range(2):
+            y_turn(0, pair)
+            y_take(0, pair, "S")
+        for a in range(4, 8):
+            y_round(0, a, "G")
+        for a in range(4):
+            out_product(1, a)
+        y_quantise(0, 0, 512)
+        store_words(0, 0, 512)
+        for pair in range(2, 4):
+            y_turn(0, pair)
+            y_take(0, pair, "SV"[pair % 2])
+        y_quantise(0, 512, 1024)
+        store_words(0, 512, 1024)
+        store_scales(0)
+        for a in range(4):
+            y_round(1, a, "GV"[a % 2])
+
+        for a in range(6, 8):
+            y_direct_product(1, a)
+            y_direct_take(1, a, "SV"[a % 2])
+        for a in range(4, 6):
+            out_product(1, a)
+            y_round(1, a, "V")
+        y_quantise(1, 768, 1024)
+        for pair in range(2):
+            y_turn(1, pair)
+            y_take(1, pair, "VS"[pair])
+        y_quantise(1, 0, 512)
+        store_words(1, 0, 512)
+        out_product(1, 6)
+        y_turn(1, 2)
+        y_take(1, 2, "V")
+        out_product(1, 7)
+        y_quantise(1, 512, 768)
+        store_words(1, 512, 1024)
+        store_scales(1)

from contextlib import ExitStack

import concourse.mybir as mybir
from concourse.masks import make_identity

F32 = mybir.dt.float32
BF16 = mybir.dt.bfloat16
U8 = mybir.dt.uint8
U32 = mybir.dt.uint32
I32 = mybir.dt.int32
E4M3 = mybir.dt.float8_e4m3fn_x4
E2M1 = mybir.dt.float4_e2m1fn_x4
ADD = mybir.AluOpType.add
MULT = mybir.AluOpType.mult
ACT = mybir.ActivationFunctionType

P = 128
PACK = 4
PASS = P * PACK
SIZE = 1024
HALVES = SIZE // PASS
BANK = 512
ROOT = 1.0 / 32.0

FLOPS = 3 * 2 * SIZE * SIZE * SIZE


def tile_adversarialsdfconditionalpricingmoments_x2_kernel(
    tc, z, wo_words, wo_scales, wg_words, wg_scales, bg, r, v, u, out_0, out_1, out_2
):
    nc = tc.nc
    with ExitStack() as ctx:
        keep = ctx.enter_context(tc.tile_pool(name="keep", bufs=1))
        work = ctx.enter_context(tc.tile_pool(name="work", bufs=8))
        psum = ctx.enter_context(tc.psum_pool(name="psum", bufs=4))

        def kept(name, shape, dtype):
            return keep.tile(shape, dtype, name=name, align_bytes=64)

        def kept_pair(name, shape, dtype):
            return [kept("%s_%d" % (name, i), shape, dtype) for i in range(HALVES)]

        identity = kept("identity", [P, P], F32)
        identity_8 = kept("identity_8", [P, 8], BF16)
        ones = kept("ones", [P, P], BF16)
        zero = kept("zero", [P, 1], F32)
        z_rows = kept_pair("z_rows", [P, PACK, SIZE], BF16)
        r_rows = kept_pair("r_rows", [P, PACK, SIZE], BF16)
        wo_codes = kept("wo_codes", [P, HALVES, 2 * SIZE], U8)
        wg_codes = kept("wg_codes", [P, HALVES, 2 * SIZE], U8)
        wo_bytes = kept("wo_bytes", [P, HALVES, SIZE], U8)
        wg_bytes = kept("wg_bytes", [P, HALVES, SIZE], U8)
        bg_rows = kept("bg_rows", [P, P], BF16)
        bg_col = kept("bg_col", [P, 8], F32)
        u_row = kept("u_row", [P, SIZE], BF16)
        u_all = kept("u_all", [P, HALVES, PASS], F32)
        v_col = kept("v_col", [P, HALVES, PACK], BF16)
        z_in = [kept_pair("z_in_%d" % g, [P, PASS, PACK], BF16) for g in range(HALVES)]
        z_codes = [kept_pair("z_codes_%d" % g, [P, PASS], U32) for g in range(HALVES)]
        z_bytes = [kept_pair("z_bytes_%d" % g, [P, PASS], U8) for g in range(HALVES)]
        f_in = kept_pair("f_in", [P, SIZE, PACK], BF16)
        f_codes = kept_pair("f_codes", [P, SIZE], U32)
        f_bytes = kept_pair("f_bytes", [P, SIZE], U8)
        returns = kept_pair("returns", [P, PACK, HALVES], F32)
        sdf_parts = kept_pair("sdf_parts", [P, 3, PACK], F32)
        d_rows = kept_pair("d_rows", [P, PACK, SIZE], BF16)
        d_in = kept_pair("d_in", [P, SIZE, PACK], BF16)
        d_codes = kept_pair("d_codes", [P, SIZE], U32)
        d_bytes = kept_pair("d_bytes", [P, SIZE], U8)
        y_in = kept_pair("y_in", [P, SIZE, PACK], BF16)
        y_codes = kept_pair("y_codes", [P, SIZE], U32)
        y_bytes = kept_pair("y_bytes", [P, SIZE], U8)

        def product_bank():
            return psum.tile([P, BANK], F32, name="product")

        def turn_bank(shape):
            return psum.tile(shape, F32, name="turn")

        def flat(ap):
            return ap.rearrange("p c k -> p (c k)")

        def words(ap):
            return flat(ap).bitcast(F32).rearrange("p (c e) -> p c e", e=2)

        def quantise(codes, scale_bytes, values, cols):
            nc.vector.quantize_mx(
                out=codes[:, cols].bitcast(E4M3), scales=scale_bytes[:, cols], in_=flat(values[:, cols, :])
            )

        def copy_on(engine, out, in_):
            if engine == "S":
                nc.scalar.copy(out=out, in_=in_)
            else:
                nc.vector.tensor_copy(out=out, in_=in_)

        for scale_tile in (wo_bytes, wg_bytes):
            nc.vector.memset(flat(scale_tile[:]).bitcast(I32), 0)
        nc.vector.memset(u_row[:], 0.0)
        nc.vector.memset(bg_rows[:], 0.0)
        nc.vector.memset(ones[:], 1.0)
        nc.vector.memset(zero[:], 0.0)
        nc.scalar.activation(out=zero[:], in_=zero[:], func=ACT.Tanh)

        def load_rows(tile, src, g, j):
            rows = src[PASS * g : PASS * (g + 1), :].rearrange("(p j) n -> p j n", j=PACK)
            nc.sync.dma_start(out=tile[g][:, j : j + 2, :], in_=rows[:, j : j + 2, :])

        def load_words(tile, src):
            nc.sync.dma_start(out=tile[:].bitcast(I32), in_=src.rearrange("g p n -> p g n").bitcast(I32))

        def load_scales(queue, tile, src):
            for b in range(4):
                queue.dma_start(
                    out=tile[32 * b : 32 * b + 4, :, :].bitcast(I32),
                    in_=src[:, 4 * b : 4 * b + 4, :].rearrange("g q n -> q g n").bitcast(I32),
                )

        load_rows(z_rows, z, 0, 0)
        load_rows(z_rows, z, 0, 2)
        load_scales(nc.scalar, wo_bytes, wo_scales)
        load_words(wo_codes, wo_words)
        load_rows(r_rows, r, 0, 0)
        load_rows(r_rows, r, 0, 2)
        load_rows(z_rows, z, 1, 0)
        load_rows(z_rows, z, 1, 2)
        load_words(wg_codes, wg_words)
        load_rows(r_rows, r, 1, 0)
        load_rows(r_rows, r, 1, 2)
        make_identity(nc, identity[:])
        nc.gpsimd.dma_start(out=bg_rows[0:8, :], in_=bg.rearrange("(a p) -> a p", p=P))
        nc.gpsimd.dma_start(out=v_col[:], in_=v.rearrange("(g p j) -> p g j", p=P, j=PACK))
        nc.gpsimd.dma_start(out=u_row[0:1, :], in_=u.unsqueeze(0))
        load_scales(nc.gpsimd, wg_bytes, wg_scales)

        live = {}

        def bias_columns():
            nc.scalar.copy(out=identity_8[:], in_=identity[:, 0:8])
            bank = turn_bank([P, 8])
            nc.tensor.matmul(bank[:], bg_rows[:], identity_8[:], start=True, stop=True)
            nc.scalar.activation(out=bg_col[:], in_=bank[:], func=ACT.Identity, bias=zero[:])

        def weights_on_all_partitions():
            for g in range(HALVES):
                bank = turn_bank([P, PASS])
                nc.tensor.matmul(bank[:], ones[:], u_row[:, PASS * g : PASS * (g + 1)], start=True, stop=True)
                nc.scalar.copy(
                    out=u_all[:, g, :].rearrange("p (w c e) -> p w c e", w=2, e=2),
                    in_=bank[:].rearrange("p (c w e) -> p w c e", w=2, e=2),
                )

        def z_turn(g, c, j):
            bank = turn_bank([P, 2, 2 * P])
            z_words = flat(z_rows[g][:]).bitcast(F32).rearrange("p (j w) -> p j w", j=PACK)
            for i in range(2):
                for w in range(2):
                    nc.tensor.transpose(
                        bank[:, w, P * i : P * (i + 1)],
                        z_words[:, j + i, 2 * P * c + w : 2 * P * (c + 1) : 2],
                        identity[:],
                    )
            live["z", g, c, j] = bank

        def z_take(g, c, j, engine):
            cols = slice(P * j, P * (j + 2))
            copy_on(engine, words(z_in[g][c][:, cols, :]), live["z", g, c, j][:].rearrange("p w n -> p n w"))

        def z_quantise(g, c, j):
            quantise(z_codes[g][c], z_bytes[g][c], z_in[g][c], slice(P * j, P * (j + 2)))

        def om_product(g, j, n):
            bank = product_bank()
            cols = slice(P * j, P * (j + 1))
            for c in range(HALVES):
                nc.tensor.matmul_mx(
                    out=bank[:],
                    lhsT=z_codes[g][c][:, cols].bitcast(E4M3),
                    lhsT_scale=z_bytes[g][c][:, cols],
                    rhs=wo_codes[:, c, 2 * BANK * n : 2 * BANK * (n + 1)].bitcast(E2M1),
                    rhs_scale=wo_bytes[:, c, BANK * n : BANK * (n + 1)],
                    start=c == 0,
                    stop=c == HALVES - 1,
                )
            live["om", g, j, n] = bank

        def om_return(g, j, n):
            om_r = work.tile([P, BANK], F32, name="om_r", bufs=2)
            nc.vector.scalar_tensor_tensor(
                out=om_r[:],
                in0=live["om", g, j, n][:],
                scalar=1.0,
                in1=r_rows[g][:, j, BANK * n : BANK * (n + 1)],
                op0=MULT,
                op1=MULT,
                accum_out=returns[g][:, j, n : n + 1],
            )

        def sdf_weight(g):
            total, sdf, v_sdf = (sdf_parts[g][:, i, :] for i in range(3))
            nc.gpsimd.tensor_tensor(out=total, in0=returns[g][:, :, 0], in1=returns[g][:, :, 1], op=ADD)
            nc.gpsimd.tensor_scalar(out=sdf, in0=total, scalar1=-ROOT, scalar2=1.0, op0=MULT, op1=ADD)
            nc.gpsimd.tensor_tensor(out=v_sdf, in0=sdf, in1=v_col[:, g, :], op=MULT)

        def d_scale(g):
            for j in range(PACK):
                nc.vector.tensor_scalar(
                    out=d_rows[g][:, j, :],
                    in0=r_rows[g][:, j, :],
                    scalar1=sdf_parts[g][:, 2, j : j + 1],
                    scalar2=None,
                    op0=MULT,
                )

        def d_interleave(g, quarter, engine):
            cols = slice(2 * P * quarter, 2 * P * (quarter + 1))
            copy_on(engine, d_in[g][:, cols, :], d_rows[g][:, :, cols].rearrange("p j n -> p n j"))

        def d_quantise(g, a0, a1):
            quantise(d_codes[g], d_bytes[g], d_in[g], slice(a0, a1))

        def x_product(g, a):
            bank = product_bank()
            for c in range(HALVES):
                nc.tensor.matmul_mx(
                    out=bank[:],
                    lhsT=wg_codes[:, c, 2 * P * a : 2 * P * (a + 1)].bitcast(E2M1),
                    lhsT_scale=wg_bytes[:, c, P * a : P * (a + 1)],
                    rhs=z_codes[g][c][:].bitcast(E4M3),
                    rhs_scale=z_bytes[g][c][:],
                    start=c == 0,
                    stop=c == HALVES - 1,
                )
            tanh_x = work.tile([P, PASS], F32, name="tanh_x", bufs=12)
            nc.scalar.activation(out=tanh_x[:], in_=bank[:], func=ACT.Tanh, bias=bg_col[:, a : a + 1])
            live["tanh", g, a] = tanh_x

        def f_scale(g, a):
            f_t = work.tile([P, PASS], BF16, name="f_t")
            nc.vector.tensor_tensor(
                out=f_t[:].rearrange("q (w p e) -> q w p e", w=2, e=2),
                in0=live["tanh", g, a][:].rearrange("q (w e p) -> q w p e", w=2, e=2),
                in1=u_all[:, g, :].rearrange("q (w p e) -> q w p e", w=2, e=2),
                op=MULT,
            )
            live["f", g, a] = f_t

        def words_turn(first, second):
            bank = turn_bank([P, 2, 2 * P])
            for i, tile in enumerate((first, second)):
                pairs = tile[:].bitcast(F32)
                for w in range(2):
                    nc.tensor.transpose(bank[:, w, P * i : P * (i + 1)], pairs[:, P * w : P * (w + 1)], identity[:])
            return bank

        def f_turn(g, pair):
            live["f turned", g, pair] = words_turn(live["f", g, 2 * pair], live["f", g, 2 * pair + 1])

        def f_take(g, pair, engine):
            cols = words(f_in[g][:]).rearrange("p (h j m b) w -> p h m j b w", h=2, j=PACK, m=2)
            bank = live["f turned", g, pair][:].rearrange("p w (b j) -> p j b w", j=PACK)
            copy_on(engine, cols[:, pair // 2, pair % 2, :, :, :], bank)

        def f_quantise(g, h):
            quantise(f_codes[g], f_bytes[g], f_in[g], slice(PASS * h, PASS * (h + 1)))

        def out_product(h, a):
            bank = product_bank()
            rows, cols = slice(P * a, P * (a + 1)), slice(PASS * h, PASS * (h + 1))
            for g in range(HALVES):
                nc.tensor.matmul_mx(
                    out=bank[:],
                    lhsT=d_codes[g][:, rows].bitcast(E4M3),
                    lhsT_scale=d_bytes[g][:, rows],
                    rhs=f_codes[g][:, cols].bitcast(E4M3),
                    rhs_scale=f_bytes[g][:, cols],
                    start=g == 0,
                    stop=g == HALVES - 1,
                )
            y = work.tile([P, PASS], F32, name="y")
            nc.scalar.mul(
                out=y[:].rearrange("i (p j) -> i p j", j=PACK),
                in_=bank[:].rearrange("i (j p) -> i p j", j=PACK),
                mul=ROOT,
            )
            nc.sync.dma_start(out=out_0[rows, cols], in_=y[:])
            live["y", h, a] = y

        def y_round(h, a, engine):
            y_t = work.tile([P, PASS], BF16, name="y_t")
            rounded = y_t[:].rearrange("i (w p e) -> i w p e", w=2, e=2)
            exact = live["y", h, a][:].rearrange("i (p w e) -> i w p e", w=2, e=2)
            if engine == "G":
                nc.gpsimd.tensor_scalar(out=rounded, in0=exact, scalar1=1.0, scalar2=0.0, op0=MULT, op1=ADD)
            else:
                nc.vector.tensor_copy(out=rounded, in_=exact)
            live["y rounded", h, a] = y_t

        def y_turn(h, pair):
            live["y turned", h, pair] = words_turn(
                live["y rounded", h, 2 * pair], live["y rounded", h, 2 * pair + 1]
            )

        def y_take(h, pair, engine):
            cols = slice(2 * P * pair, 2 * P * (pair + 1))
            copy_on(engine, words(y_in[h][:, cols, :]), live["y turned", h, pair][:].rearrange("p w n -> p n w"))

        def y_direct_product(h, a):
            bank = turn_bank([P, PACK, P])
            rows = slice(P * a, P * (a + 1))
            for j in range(PACK):
                cols = slice(PASS * h + P * j, PASS * h + P * (j + 1))
                for g in range(HALVES):
                    nc.tensor.matmul_mx(
                        out=bank[:, j, :],
                        lhsT=f_codes[g][:, cols].bitcast(E4M3),
                        lhsT_scale=f_bytes[g][:, cols],
                        rhs=d_codes[g][:, rows].bitcast(E4M3),
                        rhs_scale=d_bytes[g][:, rows],
                        start=g == 0,
                        stop=g == HALVES - 1,
                    )
            live["y direct", h, a] = bank

        def y_direct_take(h, a, engine):
            out = y_in[h][:, P * a : P * (a + 1), :]
            bank = live["y direct", h, a][:].rearrange("p j n -> p n j")
            if engine == "S":
                nc.scalar.mul(out=out, in_=bank, mul=ROOT)
            else:
                nc.vector.tensor_scalar(out=out, in0=bank, scalar1=ROOT, scalar2=None, op0=MULT)

        def y_quantise(h, a0, a1):
            quantise(y_codes[h], y_bytes[h], y_in[h], slice(a0, a1))

        def store_words(h, a0, a1):
            nc.sync.dma_start(
                out=flat(out_1[h])[:, PACK * a0 : PACK * a1].bitcast(I32), in_=y_codes[h][:, a0:a1].bitcast(I32)
            )

        def store_scales(h):
            for b in range(4):
                nc.sync.dma_start(
                    out=out_2[h, 4 * b : 4 * b + 4, :].bitcast(I32),
                    in_=y_bytes[h][32 * b : 32 * b + 4, :].bitcast(I32),
                )

        om_steps = [(j, n) for j in range(PACK) for n in range(HALVES)]

        def z_half(g, engines):
            for j in (0, 2):
                for c in range(HALVES):
                    z_turn(g, c, j)
                    z_take(g, c, j, engines[c])
                for c in range(HALVES):
                    z_quantise(g, c, j)

        z_half(0, "SV")
        for i, step in enumerate(om_steps):
            om_product(0, *step)
            om_return(0, *step)
            if i == 3:
                bias_columns()
                weights_on_all_partitions()
        sdf_weight(0)
        z_half(1, "SS")
        d_scale(0)

        for a in range(4):
            x_product(0, a)
        for a in range(4):
            f_scale(0, a)
        for a in range(4):
            for step in om_steps[2 * a : 2 * a + 2]:
                om_product(1, *step)
                om_return(1, *step)
            x_product(1, a)
            if a > 0:
                f_scale(1, a - 1)
            d_interleave(0, a, "S")
            if a == 1:
                for pair in range(2):
                    f_turn(0, pair)
                for pair in range(2):
                    f_take(0, pair, "S")
        sdf_weight(1)
        f_scale(1, 3)
        d_scale(1)

        for a in range(4, 6):
            x_product(0, a)
        d_interleave(1, 0, "S")
        for pair in range(2):
            f_turn(1, pair)
        d_interleave(1, 1, "V")
        for pair in range(2):
            f_take(1, pair, "VS"[pair])
        f_quantise(0, 0)
        d_quantise(0, 0, 512)
        d_quantise(1, 256, 512)
        d_quantise(1, 0, 256)
        f_quantise(1, 0)
        for a in range(6, 8):
            x_product(0, a)
        for a in range(4, 6):
            x_product(1, a)
        d_interleave(1, 2, "S")
        for a in range(4, 8):
            f_scale(0, a)
        for a in range(4):
            out_product(0, a)
        d_quantise(0, 512, 1024)
        d_interleave(1, 3, "V")
        d_quantise(1, 512, 1024)
        for a in range(6, 8):
            x_product(1, a)
        for pair in range(2, 4):
            f_turn(0, pair)
        for pair in range(2, 4):
            f_take(0, pair, "VS"[pair % 2])
        for a in range(4, 8):
            f_scale(1, a)
        for a in range(4, 8):
            out_product(0, a)
        for a in range(4):
            y_round(0, a, "G")
        f_quantise(0, 1)
        for pair in range(2, 4):
            f_turn(1, pair)
        for pair in range(2, 4):
            f_take(1, pair, "VS"[pair % 2])
        f_quantise(1, 1)

        for pair in range(2):
            y_turn(0, pair)
            y_take(0, pair, "S")
        for a in range(4, 8):
            y_round(0, a, "G")
        for a in range(4):
            out_product(1, a)
        y_quantise(0, 0, 512)
        store_words(0, 0, 512)
        for pair in range(2, 4):
            y_turn(0, pair)
            y_take(0, pair, "SV"[pair % 2])
        y_quantise(0, 512, 1024)
        store_words(0, 512, 1024)
        store_scales(0)
        for a in range(4):
            y_round(1, a, "GV"[a % 2])

        for a in range(6, 8):
            y_direct_product(1, a)
            y_direct_take(1, a, "SV"[a % 2])
        for a in range(4, 6):
            out_product(1, a)
            y_round(1, a, "V")
        y_quantise(1, 768, 1024)
        for pair in range(2):
            y_turn(1, pair)
            y_take(1, pair, "VS"[pair])
        y_quantise(1, 0, 512)
        store_words(1, 0, 512)
        out_product(1, 6)
        y_turn(1, 2)
        y_take(1, 2, "V")
        out_product(1, 7)
        y_quantise(1, 512, 768)
        store_words(1, 512, 1024)
        store_scales(1)
